import numpy as np, ml_dtypes
CORES = [16,17,18,19,32,33,34,35]
N = 8
import mx_ref
BF = ml_dtypes.bfloat16
def tile(rs):
    return np.stack(rs, axis=2).reshape(128, -1).astype(BF)
def pick(q, e):
    c = np.concatenate([q[0].reshape(128, -1, 4), np.zeros((128, 1, 4), np.uint8)], axis=1); s = np.concatenate([q[1], np.ones((16, 1), np.uint8)], axis=1)
    return (np.ascontiguousarray(c[:, e].reshape(128, -1)), np.ascontiguousarray(s[:, e]))
def join(*qs):
    return (np.concatenate([q[0] for q in qs], axis=1), np.concatenate([q[1] for q in qs], axis=1))
def put(q, e, v):
    c, s = q[0].reshape(128, -1, 4).copy(), q[1].copy(); c[:, e] = v[0].reshape(128, -1, 4); s[:, e] = v[1]
    return (c.reshape(128, -1), s)
def pk(c, s):
    return (np.ascontiguousarray(c), mx_ref.live(s))
def emit(q):
    return q[0], q[1]
def packed(v, rng):
    q = [mx_ref.quantize(np.ascontiguousarray(v[r])) for r in range(N)]
    return np.stack([a for a, b in q]), np.stack([mx_ref.plane(b, rng) for a, b in q])
def values_of_codes():
    e, c = np.zeros((128, 128, 4), np.float32), np.zeros((128, 2, 4), np.uint8)
    e[np.arange(128), np.arange(128), 0] = 1
    c[:127, :, 0] = np.arange(256).reshape(2, 128).T[:127]
    return mx_ref.matmul(mx_ref.quantize(e.reshape(128, 512).astype(BF)), (c.reshape(128, 8), np.full((16, 2), 127, np.uint8))).T.reshape(-1).astype(np.float64)
CODE_VALUE, SCALE_VALUE = values_of_codes(), 2.0 ** (np.arange(256) - 127.0)
def decode(q):
    return (CODE_VALUE[q[0]].reshape(16, 8, -1, 4) * SCALE_VALUE[q[1]][:, None, :, None] + 0.0).reshape(128, -1).astype(np.float32)
def f(rng, *shape):
    return mx_ref.flush((rng.standard_normal(shape, dtype=np.float32) * np.exp2(rng.integers(-2, 3, shape[:-1] + (1,)))).astype(BF))
def wide(rng, *shape, cols=0):
    v = rng.standard_normal(shape, dtype=np.float32) * np.exp2(rng.integers(-12, 13, shape)).astype(np.float32)
    if cols: v *= np.repeat(np.exp2(rng.integers(-cols, cols + 1, shape[:-2] + (1, shape[-1] // 4))) * (rng.random(shape[:-2] + (1, shape[-1] // 4)) > 0.0625), 4, axis=-1).astype(np.float32)
    return mx_ref.flush(v.astype(BF))
C, XOR = 320, [1, 2, 4]
def big(v):
    v = v.astype(np.float32)
    v[np.abs(v) < np.float32(2.0 ** -16)] = 0
    return v.astype(BF)
def numbers_of(rng):
    return {"x": big(f(rng, N, 128, 4 * C)), "u": np.array(f(rng, N, 128, 512)), "v": np.array(f(rng, N, 128, 512))}
def layers(rng):
    return big(f(rng, N, 128, 2048)).astype(np.float32).reshape(N, 8, 16, 4, 8, 16, 4)
def weights(rng, w):
    c, s = packed(np.ascontiguousarray(w).reshape(N, 128, 2048).astype(BF), rng)
    return {"wc": c, "ws": s}
def label(rng, d, e, k):
    x, u = d["x"].reshape(N, 8, 16, C, 4), d["u"].reshape(N, 128, 128, 4)
    d["u"].reshape(N, 128, 8, 16, 4)[:, :, :, :8] = 0
    for r in range(N):
        for g in range(8):
            o, a = rng.permutation(8), np.zeros((8, C), np.float32)
            a[o] = e[r, g]
            x[r, g, :2] = a.reshape(2, 4, C).transpose(0, 2, 1).astype(BF)
            for i in range(8): u[r, 16 * g + o[i] // 4, 16 * g + i, o[i] % 4] = float(k[r])
def setup_inputs(rng):
    return {**numbers_of(rng), **weights(rng, layers(rng))}
def setup_inputs_ties(rng):
    d = numbers_of(rng)
    o = rng.permutation(N)
    h = rng.permutation(8)[:4]
    e = rng.integers(0, 3, (N, 8, 8, C))
    e[o[2]] = 1
    e[o[3], h] = 0
    k = np.ones(N)
    k[o[0]], k[o[1]] = 0, -1
    label(rng, d, e, k)
    z = (N, 8, 8, C, 4)
    a = (1.125 + 0.25 * rng.integers(0, 4, z)) * np.exp2(rng.integers(-2, 5, z))
    a[:, :, 0, :, 0] = 1.96875 * 2.0 ** 12
    a = a * rng.choice([-1.0, 1.0], z)
    a[o[3], h, 1:3] = (1.375 + 0.25 * rng.integers(0, 2, (4, 2, C, 4))) * np.exp2(rng.integers(-2, 5, (4, 1, C, 1)))
    d["x"].reshape(N, 8, 16, C, 4)[:, :, 8:] = a.astype(np.float32).astype(BF)
    u = d["u"].reshape(N, 128, 128, 4)
    for g in h:
        for i in range(8): u[o[3], 16 * g + 9 + i // 4, 16 * g + i, i % 4] = 1.0
    w = layers(rng)
    w[:, :, 8] = 0
    w[:, :, :, :, :, [0, 1, 8]] = 0
    w[:, :, :, :, :, 9:] *= np.float32(0.125)
    return {**d, **weights(rng, w)}
def setup_inputs_near(rng):
    d = numbers_of(rng)
    x = d["x"].astype(np.float32).reshape(N, 8, 16, C, 4)
    x[:, :, :2] = 0
    x[:, :, 2:8] *= np.float32(0.125)
    x[:, :, 8:] = 0
    x[:, :, 0, :, 0] = rng.choice([-1.0, 1.0], (N, 8, C))
    x[:, :, 1, :, 0] = 2.0 ** -10
    x[:, :, 8:, :, 0] = rng.integers(0, 8, (N, 8, 8, C)) * 2.0 ** -23
    x[:, :, 8:12, :, 1] = 2.0 ** -30
    x[:, :, 12:, :, 1] = rng.choice([1.0, 1.125], (N, 8, 4, C)) * 2.0 ** -30
    u = d["u"].reshape(N, 128, 128, 4)
    d["u"].reshape(N, 128, 8, 16, 4)[:, :, :, :8] = 0
    o = rng.permutation(N) % 4
    for r in range(N):
        for g in rng.permutation(8)[:4]: x[r, g, 8 + rng.integers(8), rng.integers(C), 0] = 2.0 ** 14
        for h in range(0, 128, 16):
            far = int(rng.integers(8))
            for i in range(8):
                k = 1.0 if o[r] == 0 else 2.0 ** -30
                if o[r] < 2: u[r, h:h + 2, h + i, 0] = k
                if o[r] == 2 and i == far: u[r, h + 1, h + i, 0] = -1.0
                elif o[r] < 3: u[r, h + 8 + i, h + i, 0] = k
                else: u[r, h + 8 + i, h + i, 1] = k * 1.25 if i < 4 else k * 1.125
    w = layers(rng)
    for i in (0, 1, 8, 9, 10, 11, 12, 13, 14, 15):
        w[:, :, i] = 0
        w[:, :, :, :, :, i] = 0
    return {"x": x.reshape(N, 128, 4 * C).astype(BF), "u": d["u"], "v": d["v"], **weights(rng, w)}
def setup_inputs_huge(rng):
    d = numbers_of(rng)
    o = rng.permutation(N)
    a = rng.permuted(np.tile(np.repeat([2.0 ** 29, 2.0 ** 30], 256), (N, 64, 1)), axis=2).reshape(N, 8, 8, 512)
    for r in range(N):
        if o[r] < N // 2: a[r] *= (rng.permutation(8) % 2 * 2.0 - 1.0)[:, None, None]
        else:
            for g in range(8): a[r, g] *= (rng.permutation(8) % 2 * 2.0 - 1.0)[:, None]
    d["u"].reshape(N, 128, 8, 16, 4)[:, :, :, :8] = a.reshape(N, 8, 8, 128, 4).transpose(0, 3, 1, 2, 4).astype(np.float32).astype(BF)
    d["x"] = ((0.2 + 0.5 * rng.random((N, 128, 4 * C))) * 2.0 ** 29).astype(np.float32).astype(BF)
    return {**d, **weights(rng, layers(rng) * np.float32(2.0 ** -8))}
def setup_inputs_ends(rng):
    d = numbers_of(rng)
    o = rng.permutation(N) % 4
    z, k = np.where(o % 2 == 0, 2.0 ** 30, 2.0 ** -30), np.where(o < 2, 2.0 ** 30, 2.0 ** -30)
    s = rng.choice([-1.0, 1.0], (N, 128, 4 * C))
    s[o == 0] = 1.0
    d["x"] = (s * z[:, None, None]).astype(np.float32).astype(BF)
    for n in ("u", "v"): d[n] = (rng.choice([-1.0, 1.0], (N, 128, 512)) * k[:, None, None]).astype(np.float32).astype(BF)
    counts = [[3 * C + 1, 3 * C - 1, C, C - 1, 1, 0, 0, 0], [8 * C] + [0] * 7, [C] * 8, [C + 1, C - 1] + [C] * 6]
    e, i, low = np.zeros((N, 8, 8, C)), np.arange(8)[None, :, None], {}
    for r in range(N):
        if o[r] == 0:
            m, h, j = np.insert(rng.permutation(7) + 1, 2, 0), int(rng.integers(8)), int(rng.integers(C // 4))
            c = np.zeros((8, C), int)
            c[h] = m[0]
            c[np.ix_(np.delete(np.arange(8), h), np.delete(np.arange(C), j))] = rng.permutation(np.repeat(m, np.array(counts[0]) - np.array([C, 0, 7, 0, 0, 0, 0, 0]))).reshape(7, C - 1)
            c = c.reshape(8, 1, C)
            low[r] = (h, int(m[0]), j)
        else: c = rng.permutation(np.repeat(rng.permutation(8), counts[o[r]])).reshape(8, 1, C)
        equal = (rng.permutation(8) < 4)[:, None, None] & (rng.random((8, 8, C)) < 0.5)
        e[r] = np.where((i == c) | (i > c) & equal, z[r], -z[r])
    for r in low:
        e[r, low[r][0]] = z[r]
        e[r, :, :, low[r][2]] = z[r]
    label(rng, d, e, k)
    for r in low:
        h, m = low[r][:2]
        a = d["u"].reshape(N, 8, 16, 8, 16, 4)[r]
        a[:, 2:, :, :8] = -2.0 ** 30
        a[:, :, h, :8] = -2.0 ** 30
        a[h, 2, h, m, 0] = 0
    return {**d, **weights(rng, np.zeros((N, 128, 2048), np.float32))}
def setup_inputs_spread(rng):
    d = numbers_of(rng)
    d["x"] = big(wide(rng, N, 128, 4 * C, cols=6))
    return {**d, **weights(rng, layers(rng) * np.float32(0.25))}
def check_inputs(d):
    b = []
    for k in ("x", "u", "v"):
        a = np.abs(d[k].astype(np.float32))
        if not (np.isfinite(a).all() and ((a == 0) | (a >= 2.0 ** -30) & (a <= 2.0 ** 30)).all()): b.append("a value of " + k)
    none, least, most = [emit(mx_ref.quantize(np.full((128, 16), k, np.float32).astype(BF)))[1][0, 0] for k in (0.0, 2.0 ** -30, 2.0 ** 30)]
    m, t = float(np.max(np.abs(d["x"].astype(np.float32)))), 0.0
    for r in range(N):
        if ((d["wc"][r] == 0x7F) | (d["wc"][r] == 0xFF)).any(): b.append("wc: a code that is no number")
        s = mx_ref.live(d["ws"][r])
        if ((s != none) & ((s < least) | (s > most))).any(): b.append("ws: a scale out of range")
        w = np.abs(decode(pk(d["wc"][r], d["ws"][r]))).astype(np.float64).reshape(128, 512, 4)
        t = max(t, float(np.max(np.sum(w, axis=(0, 2)))))
    if not (t == 0 or m * (1 + t * 0.015625) ** 3 <= 2.0 ** 29): b.append("m * (1 + s * 0.015625)**3 is beyond 2**29, and s isn't 0")
    return b
def sources(c):
    e, over = np.full((8, C), -1), []
    for k in range(8):
        w = np.flatnonzero(c == k)
        e[k, :min(len(w), C)] = w[:C]
        over.append(w[C:])
    e[e < 0] = np.sort(np.concatenate(over))
    return e
def reference(x, u, v, wc, ws):
    qu = [mx_ref.quantize(u[r]) for r in range(N)]
    lay = [pk(wc[r], ws[r]) for r in range(N)]
    now = [x[r] for r in range(N)]
    y, om = np.zeros((N, 128, C), np.float32), np.zeros((N, 8, C), np.float32)
    oc, osc = np.zeros((N, 128, 4 * C), np.uint8), np.zeros((N, 16, C), np.uint8)
    for a in XOR:
        kept, sent = [], []
        for r in range(N):
            q = mx_ref.quantize(now[r])
            s = mx_ref.matmul(qu[r], q).reshape(8, 16, C)[:, :8] + np.float32(0.0)
            e = sources(np.argmax(s, axis=1).T.reshape(-1))
            t = decode(q).reshape(8, 16, C, 4).transpose(0, 2, 1, 3)
            made = t[e % 8, e // 8].transpose(0, 2, 1, 3).reshape(128, 4 * C).astype(BF)
            kept.append(made[:, :2 * C])
            sent.append(mx_ref.quantize(np.ascontiguousarray(made[:, 2 * C:])))
            om[r] = e
        for r in range(N):
            z = np.concatenate([kept[r], decode(sent[r ^ a]).astype(BF)], axis=1)
            q = mx_ref.quantize(z)
            now[r] = tile([mx_ref.matmul(pick(lay[r], np.arange(128 * b, 128 * b + 128)), q) * np.float32(0.015625) + z[:, b::4].astype(np.float32) for b in range(4)])
    for r in range(N):
        q = mx_ref.quantize(now[r])
        y[r] = mx_ref.matmul(mx_ref.quantize(v[r]), q)
        oc[r], osc[r] = emit(q)
    return {"y": y, "om": om, "oc": oc, "osc": osc}

@@ -1,0 +1,364 @@
+from concourse.mybir import dt, AluOpType as A, ActivationFunctionType as AF
+
+ROUNDS = [1, 2, 4]
+BIG = float(2.0 ** 75)
+EC = 192
+SCRATCH = {}
+for _d, _l in {"bfloat16": "xt 1280 yt 1280 y64 640 ut 512 vt 512 dg 192 et 3072 on 128 la 128 lb 128 lm 1024 hu 560 tw 10240",
+               "float32": "st 320 fm 320 rst 160 mk 96 zf 256 occ 8 fr 8 fb 8 wv 8 w0 8 val 320 win0 4096 win1 4096 win2 4096 "
+                          "w3 20 ng 20 sv 20 cc 2 gt 20 n8 20 nn 32 omt 32 yo 320 t64 640",
+               "int32": "pj 2 pk 2 gi 20", "uint16": "sl 20 gl 20"}.items():
+    _l = _l.split()
+    for _n, _w in zip(_l[::2], _l[1::2]):
+        SCRATCH[_n] = ("sbuf", [128, int(_w)], _d)
+for _n, _a, _b in (("hd", 2, 96), ("rr", 2, 96), ("sa", 2, 48), ("sb", 2, 24), ("am", 4, 96), ("am1", 4, 48), ("am2", 4, 24), ("am3", 4, 12),
+                   ("gb", 16, 12), ("gb1", 8, 12), ("gb2", 4, 12), ("wm", 8, 32), ("w1", 4, 20), ("w2", 2, 20)):
+    SCRATCH[_n] = ("sbuf", [128, _a, _b], "float32")
+for _n in "sc cb nc fp ff rj ac pa pb pc pd t0".split():
+    SCRATCH[_n] = ("sbuf", [128, 2, 12], "float32")
+for _n in "pi b0 b1 b2 b3 b4".split():
+    SCRATCH[_n] = ("sbuf", [128, 2, 12], "int32")
+for _n, _s, _w in [("xq", "xs", 320), ("uq", "us", 128), ("vq", "vs", 128), ("wq", "wsc", 512), ("eq", "es", 4 * EC), ("lq", "lqs", 256),
+                   ("hq", "hs", 140), ("zq", "zs", 160)] + [(_k + "c%d" % _t, _k + "s%d" % _t, 160) for _t in range(3) for _k in "al"]:
+    SCRATCH[_n] = ("sbuf", [128, _w], "float8_e4m3fn_x4")
+    SCRATCH[_s] = ("sbuf", [128, _w], "uint8")
+for _t in range(8):
+    SCRATCH["p%d" % _t] = ("psum", [128, 512], "float32")
+SEMAPHORES = ["qv", "qt", "qa", "qp", "dx0", "dx1", "du", "dv", "dw", "dz", "rota", "rotb", "lst", "outs",
+              "arr0", "arr1", "arr2", "snt0", "snt1", "snt2"]
+ALL = 1 << 20
+
+
+def rank_program(g, core, T, topo):
+    rank = T.rank_of(core)
+    if rank is None:
+        return
+    V, P, S, Y = g.vector, g.tensor, g.scalar, g.sync
+    queue = {"v": V, "t": P, "a": S, "s": Y, "p": g}
+    own = {"v": "qv", "t": "qt", "a": "qa", "p": "qp"}
+    cnt, clock, snap = {}, {q: {} for q in queue}, {}
+    wrote, read = {}, {}
+
+    def rg(name, lo=0, hi=ALL, step=1):
+        return (name, lo, hi, step)
+
+    def meet(a, b):
+        if a[1] >= b[2] or b[1] >= a[2]:
+            return False
+        return not (a[3] == b[3] and a[3] > 1 and (a[1] - b[1]) % a[3] != 0)
+
+    def need(rd, wr):
+        d = []
+        for r in rd:
+            d += [t for (x, t) in wrote.get(r[0], []) if meet(r, x)]
+        for r in wr:
+            d += [t for (x, t) in wrote.get(r[0], []) + read.get(r[0], []) if meet(r, x)]
+        return d
+
+    def wait(q, toks):
+        top = {}
+        for s, v in toks:
+            top[s] = max(top.get(s, 0), v)
+        for s in list(top):
+            implied = any(o != s and snap[(o, top[o])].get(s, 0) >= top[s] for o in top)
+            if not implied and clock[q].get(s, 0) < top[s]:
+                queue[q].wait_ge(T.sem[s], top[s])
+        for s, v in top.items():
+            for o, w in snap[(s, v)].items():
+                clock[q][o] = max(clock[q].get(o, 0), w)
+            clock[q][s] = max(clock[q].get(s, 0), v)
+
+    def note(tok, rd, wr):
+        for r in wr:
+            for tab in (wrote, read):
+                tab[r[0]] = [(x, t) for (x, t) in tab.get(r[0], [])
+                             if not (r[1] <= x[1] and x[2] <= r[2] and (r[3] == 1 or (r[3] == x[3] and (r[1] - x[1]) % r[3] == 0)))]
+            wrote[r[0]].append((r, tok))
+        for r in rd:
+            read.setdefault(r[0], []).append((r, tok))
+
+    def norm(l):
+        return [rg(x) if isinstance(x, str) else x for x in l]
+
+    def op(q, fn, rd, wr, free=()):
+        rd, wr, s = norm(rd), norm(wr), own[q]
+        n = cnt.get(s, 0)
+        wait(q, need(rd, [r for r in wr if r[0] not in free]) + ([(s, n)] if q == "p" and n else []))
+        cnt[s] = n + 1
+        tok = (s, n + 1)
+        snap[tok] = dict(clock[q])
+        fn().then_inc(T.sem[s], 1)
+        note(tok, rd, wr)
+
+    def dmas(s, jobs):
+        cnt[s] = cnt.get(s, 0) + 16 * len(jobs)
+        tok, sn, done = (s, cnt[s]), None, []
+        for q, o, i, rd, wr in jobs:
+            rd, wr = norm(rd), norm(wr)
+            wait(q, need(rd, wr))
+            sn = dict(clock[q]) if sn is None else {k: min(v, sn.get(k, 0)) for k, v in clock[q].items()}
+            queue[q].dma_start(o, i).then_inc(T.sem[s], 16)
+            done.append((rd, wr))
+        snap[tok] = sn
+        for rd, wr in done:
+            note(tok, rd, wr)
+
+    def mm(bank, n, lhs, rhs, rd, start=True, stop=True):
+        out = T["p%d" % bank][:, 0:n]
+        op("t", lambda: P.matmul_mx(out, lhs[0], lhs[1], rhs[0], rhs[1], start, stop), rd, ["p%d" % bank],
+           () if start else ("p%d" % bank,))
+
+    pool = [0]
+
+    def bank():
+        pool[0] += 1
+        return 2 + pool[0] % 6
+
+    def tt(o, a, b, k, rd, wr):
+        op("v", lambda: V.tensor_tensor(o, a, b, k), rd, wr)
+
+    def ts(o, a, s1, s2, rd, wr, k0, k1=None):
+        if k1 is None:
+            op("v", lambda: V.tensor_scalar(o, a, s1, None, k0), rd, wr)
+        else:
+            op("v", lambda: V.tensor_scalar(o, a, s1, s2, k0, k1), rd, wr)
+
+    def act(o, i, rd, wr, scale=1.0):
+        op("a", lambda: S.activation(o, i, AF.Copy, scale=scale), rd, wr)
+
+    def fill(ap, c, wr):
+        op("v", lambda: V.memset(ap, c), [], wr)
+
+    def quant(q, s, i, rd, wr):
+        op("v", lambda: V.quantize_mx(q, s, i), rd, wr)
+
+    dmas("dx0", [("s", T.xt[:, 0:640], T.x[:, 0:640], [], [rg("xt", 0, 640)])])
+    dmas("du", [("a", T.ut[:], T.u[:], [], ["ut"])])
+    dmas("dx1", [("s", T.xt[:, 640:1280], T.x[:, 640:1280], [], [rg("xt", 640, 1280)])])
+
+    flag = {"allow_small_or_imprecise_dtypes": True}
+    quarters = [(a, slice(32 * a, 32 * a + 32)) for a in range(4)]
+    fill(T.dg[:], 0.0, ["dg"])
+    fill(T.on[:], 1.0, ["on"])
+    for b in range(4):
+        fill(T.et[:, 4 * EC * b:4 * EC * (b + 1)], 0.0, [rg("et", 4 * EC * b, 4 * EC * (b + 1))])
+    fill(T.hu[:], 0.0, ["hu"])
+    for k in (0, 128):
+        op("p", lambda: g.affine_select(T.dg[:], T.dg[:], [[-1, EC]], A.not_equal, 64.0, k, 1), ["dg"], ["dg"])
+    for a, p in quarters:
+        op("p", lambda: g.affine_select(T.la[p, :], T.on[p, :], [[1, 4], [4, 32]], A.is_gt, 0.0, -a, -4), ["on"], [rg("la", a, a + 1)])
+    op("p", lambda: g.iota(T.zf[:], [[0, 256]], 0, 0, **flag), [], ["zf"])
+    op("p", lambda: g.affine_select(T.rst[:], T.zf[:, 0:160], [[0, 10], [1, 16]], A.not_equal, -BIG, 0, 0), ["zf"], ["rst"])
+    op("p", lambda: g.affine_select(T.mk[:], T.zf[:, 0:96], [[0, 8], [1, 12]], A.is_equal, 1.0, 0, 0), ["zf"], ["mk"])
+    for b in range(4):
+        act(T.et[:, 4 * EC * b + b:4 * EC * (b + 1):4], T.dg[:], ["dg"], [rg("et", 4 * EC * b + b, 4 * EC * (b + 1))])
+    for a, p in quarters:
+        op("p", lambda: g.iota(T.nc[p, :, :], [[32, 2], [8192, 12]], 64 * a + 1, 256, **flag), [], [rg("nc", a, a + 1)])
+    for a, p in quarters:
+        op("p", lambda: g.iota(T.val[p, :], [[1280, 2], [32, 10], [1, 16]], 2560 * a, 1, **flag), [], [rg("val", a, a + 1)])
+    op("p", lambda: g.iota(T.pj[:], [[0, 2]], 0, 1), [], ["pj"])
+    op("p", lambda: g.iota(T.nn[:], [[0, 32]], 0, 0, **flag), [], ["nn"])
+    dmas("dz", [("s", T["win%d" % t][0:128:16, :], T.zf[:], ["zf"], ["win%d" % t]) for t in range(3)])
+    dmas("dw", [("s", T.wq[:].bitcast(dt.uint8), T.wc[:], [], ["wq"]), ("s", T.wsc[:], T.ws[:], [], ["wsc"])])
+    dmas("dv", [("s", T.vt[:], T.v[:], [], ["vt"])])
+
+    U = (T.uq[:], T.us[:])
+    CC = T.cc[:, 0:1]
+
+    def xh(h):
+        return (T.xq[:, 160 * h:160 * h + 160], T.xs[:, 160 * h:160 * h + 160])
+
+    def quant_x(h):
+        lo = 160 * h
+        quant(xh(h)[0], xh(h)[1], T.xt[:, 4 * lo:4 * lo + 640], [rg("xt", 4 * lo, 4 * lo + 640)], [rg("xq", lo, lo + 160)])
+
+    def choose_half(h):
+        lo, hi = 160 * h, 160 * h + 160
+        mm(0, 160, U, xh(h), ["uq", rg("xq", lo, hi)])
+        op("v", lambda: V.transpose(T.st[:, lo:hi], T.p0[:, 0:160]), ["p0"], [rg("st", lo, hi)])
+        op("v", lambda: V.tensor_tensor_scan(T.fm[:, lo:hi], T.rst[:], T.st[:, lo:hi], 0.0, A.add, A.max), ["rst", rg("st", lo, hi)], [rg("fm", lo, hi)])
+        for i in range(8):
+            o = 48 * (i + 1) + 20 * h
+            tt(T.hu[:, o:o + 20:2], T.fm[:, lo + i:hi:16], T.fm[:, lo + 7:hi:16], A.is_ge, [rg("fm", lo, hi)], [rg("hu", o, o + 20, 2)])
+
+    def unpack(d, lo, hi):
+        for b in range(4):
+            k = bank()
+            e = EC * b + 16 * d
+            mm(k, hi - lo, (T.eq[:, e:e + 128], T.es[:, e:e + 128]), (T.xq[:, lo:hi], T.xs[:, lo:hi]), ["eq", rg("xq", lo, hi)])
+            o = 1280 * d + 320 * b
+            act(T.tw[:, o + lo:o + hi], T["p%d" % k][:, 0:hi - lo], ["p%d" % k], [rg("tw", o + lo, o + hi)], 0.015625)
+
+    def turn(s, d):
+        lo, hi = 1280 * d, 1280 * (d + 2)
+        dmas(s, [("s", T.tw[64 * k:64 * k + 64, 5120 + lo:5120 + hi], T.tw[64 - 64 * k:128 - 64 * k, lo:hi],
+                  [rg("tw", lo, hi)], [rg("tw", 5120 + lo, 5120 + hi)]) for k in range(2)])
+
+    for b in range(4):
+        e = EC * b
+        quant(T.eq[:, e:e + EC], T.es[:, e:e + EC], T.et[:, 4 * e:4 * e + 4 * EC], [rg("et", 4 * e, 4 * e + 4 * EC)], [rg("eq", e, e + EC)])
+    ts(T.lb[:], T.la[:], -1.0, 1.0, ["la"], ["lb"], A.mult, A.add)
+    quant(T.uq[:], T.us[:], T.ut[:], ["ut"], ["uq"])
+    quant_x(0)
+    quant_x(1)
+    for t in (0, 2, 1, 3):
+        for k in range(2):
+            src = "lb" if t % 2 else "la"
+            act(T.lm[:, 512 * k + t:512 * k + 512:4], T[src][:], [src], [rg("lm", 512 * k + t, 512 * k + 512, 4)], -1.0 if k else 1.0)
+    choose_half(0)
+    choose_half(1)
+    quant(T.lq[:], T.lqs[:], T.lm[:], ["lm"], ["lq"])
+    unpack(0, 0, 320)
+    unpack(1, 0, 320)
+
+    for t in range(3):
+        W = T["win%d" % t]
+        op("v", lambda: V.tensor_copy(T.hu[:, 5:432:2], T.hu[:, 0:427:2]), [rg("hu", 0, 432, 2)], [rg("hu", 5, 433, 2)])
+        quant(T.hq[:], T.hs[:], T.hu[:], ["hu"], ["hq"])
+        mm(1, 128, (T.lq[:, 0:128], T.lqs[:, 0:128]), (T.hq[:, 12:140], T.hs[:, 12:140]), ["lq", "hq"], True, False)
+        mm(1, 128, (T.lq[:, 128:256], T.lqs[:, 128:256]), (T.hq[:, 0:128], T.hs[:, 0:128]), ["lq", "hq"], False, True)
+        for e in range(2):
+            tt(T.hd[:, e, :], T.hu[:, 48 + 2 * e:432:4], T.hu[:, 2 * e:384:4], A.subtract, [rg("hu", 0, 432, 2)], ["hd%d" % e])
+        for e in range(2):
+            tt(T.sa[:, e, :], T.hu[:, 48 + 2 * e:240:4], T.hu[:, 240 + 2 * e:432:4], A.add, [rg("hu", 0, 432, 2)], ["sa%d" % e])
+        tt(T.sb[:], T.sa[:, :, 0:24], T.sa[:, :, 24:48], A.add, ["sa0", "sa1"], ["sb"])
+        tt(T.sc[:], T.sb[:, :, 0:12], T.sb[:, :, 12:24], A.add, ["sb"], ["sc"])
+        ts(T.cb[:], T.sc[:], -16384.0, 131072.0, ["sc"], ["cb"], A.mult, A.add)
+        op("v", lambda: V.tensor_tensor_scan(T.rr[:, 0, :], T.mk[:], T.p1[:, 0:96], 0.0, A.mult, A.add), ["mk", "p1"], ["rr0"])
+        tt(T.rr[:, 1, :], T.rr[:, 0, :], T.hd[:, 0, :], A.add, ["rr0", "hd0"], ["rr1"])
+        for e in range(2):
+            tt(T.am[:, e, :], T.rr[:, e, :], T.hd[:, e, :], A.mult, ["rr%d" % e, "hd%d" % e], ["am%d" % e])
+            ts(T.am[:, 2 + e, :], T.rr[:, e, :], 320.0, 32.0, ["rr%d" % e], ["am%d" % (2 + e)], A.min, A.mult)
+        ts(T.occ[:], T.rr[:, 0, 10:96:12], 320.0, None, ["rr0"], ["occ"], A.min)
+        tt(T.am1[:], T.am[:, :, 0:48], T.am[:, :, 48:96], A.add, ["am0", "am1", "am2", "am3"], ["am_1"])
+        ts(T.fr[:], T.occ[:], -32.0, 10240.0, ["occ"], ["fr"], A.mult, A.add)
+        ts(T.wv[:], T.occ[:], 32.0, 6144.0, ["occ"], ["wv"], A.mult, A.add)
+        ts(T.w0[:], T.occ[:], 32.0, -1.0, ["occ"], ["w0"], A.mult, A.add)
+        tt(T.am2[:], T.am1[:, :, 0:24], T.am1[:, :, 24:48], A.add, ["am_1"], ["am_2"])
+        op("v", lambda: V.tensor_tensor_scan(T.fb[:], T.fr[:], T.zf[:, 0:8], 1.0, A.add, A.add), ["fr", "zf"], ["fb"])
+        tt(T.am3[:], T.am2[:, :, 0:12], T.am2[:, :, 12:24], A.add, ["am_2"], ["am_3"])
+        CS, MS = T.am3[:, 0:2, :], T.am3[:, 2:4, :]
+        tt(T.fp[:], T.nc[:], MS, A.subtract, ["nc", "am_3"], ["fp"])
+        ts(T.rj[:], CS, 320.0, None, ["am_3"], ["rj"], A.is_ge)
+        ts(T.pa[:], CS, 32.0, None, ["am_3"], ["pa"], A.mult)
+        ts(T.ac[:], CS, 320.0, None, ["am_3"], ["ac"], A.is_lt)
+        tt(T.ff[:], T.fp[:], T.rj[:], A.mult, ["fp", "rj"], ["ff"])
+        tt(T.pb[:], T.pa[:], T.cb[:], A.add, ["pa", "cb"], ["pb"])
+        ts(T.t0[:], T.rj[:], T.w0[:, 0:1], None, ["rj", "w0"], ["t0"], A.mult)
+        for c in range(1, 8):
+            ts(T.gb[:, 2 * c:2 * c + 2, :], T.ff[:], T.fb[:, c - 1:c], T.wv[:, c:c + 1], ["ff", "fb", "wv"], ["gb%d" % c], A.is_ge, A.mult)
+            if c == 2:
+                tt(T.pc[:], T.pb[:], T.ac[:], A.mult, ["pb", "ac"], ["pc"])
+            if c == 4:
+                tt(T.pd[:], T.pc[:], T.t0[:], A.add, ["pc", "t0"], ["pd"])
+            if c == 6:
+                tt(T.gb[:, 0:2, :], T.ff[:], T.pd[:], A.add, ["ff", "pd"], ["gb0"])
+        tt(T.gb1[:], T.gb[:, 0:8, :], T.gb[:, 8:16, :], A.add, ["gb%d" % c for c in range(8)], ["gb_1"])
+        tt(T.gb2[:], T.gb1[:, 0:4, :], T.gb1[:, 4:8, :], A.add, ["gb_1"], ["gb_2"])
+        tt(T.pi[:], T.gb2[:, 0:2, :], T.gb2[:, 2:4, :], A.add, ["gb_2"], ["pi"])
+        ts(T.b0[:], T.pi[:], 480, None, ["pi"], ["b0"], A.bitwise_and)
+        ts(T.b1[:], T.pi[:], 5, 3584, ["pi"], ["b1"], A.arith_shift_right, A.bitwise_and)
+        ts(T.b2[:], T.pi[:], 9, 31, ["pi"], ["b2"], A.arith_shift_right, A.bitwise_and)
+        tt(T.b3[:], T.b0[:], T.b1[:], A.add, ["b0", "b1"], ["b3"])
+        tt(T.b4[:], T.b3[:], T.b2[:], A.add, ["b3", "b2"], ["b4"])
+        for e in range(2):
+            op("v", lambda: V.tensor_copy(T.sl[:, 10 * e:10 * e + 10], T.b4[:, e, 0:10]), ["b4"], [rg("sl", 10 * e, 10 * e + 10)])
+        op("v", lambda: V.tensor_copy(W[:].indirect(T.sl[:]), T.val[:]), ["sl", "val"], ["win%d" % t])
+        turn("rota", 0)
+        unpack(2, 0, 320)
+        unpack(3, 0, 320)
+        turn("rotb", 2)
+        dmas("lst", [("as"[x % 2], T.wm[:, x, :], W[16 * x:16 * x + 1, :], ["win%d" % t], ["wm%d" % x]) for x in range(8)])
+        if t == 0:
+            quant(T.vq[:], T.vs[:], T.vt[:], ["vt"], ["vq"])
+            ts(T.pk[:], T.pj[:], 4, None, ["pj"], ["pk"], A.arith_shift_right)
+            ts(T.cc[:], T.pk[:], 1280.0, None, ["pk"], ["cc"], A.mult)
+        tt(T.w1[:], T.wm[:, 0:4, 0:20], T.wm[:, 4:8, 0:20], A.add, ["wm%d" % x for x in range(8)], ["w1"])
+        tt(T.w2[:], T.w1[:, 0:2, :], T.w1[:, 2:4, :], A.add, ["w1"], ["w2"])
+        tt(T.w3[:], T.w2[:, 0, :], T.w2[:, 1, :], A.add, ["w2"], ["w3"])
+        ts(T.ng[:], T.w3[:], CC, 10240.0, ["w3", "cc"], ["ng"], A.is_lt, A.mult)
+        tt(T.sv[:], T.w3[:], T.ng[:], A.add, ["w3", "ng"], ["sv"])
+        ts(T.gl[:], T.sv[:], CC, None, ["sv", "cc"], ["gl"], A.subtract)
+
+        def gather(h):
+            for b in (0, 2, 1, 3):
+                o = T.yt[:, 640 * h + b:640 * h + 640:4]
+                i = T.tw[:, 320 * b:320 * b + 9280].indirect(T.gl[:, 10 * h:10 * h + 10])
+                rd, wr = ["gl", rg("tw", 320 * b, 320 * b + 9280)], [rg("yt", 640 * h + b, 640 * h + 640, 4)]
+                if b < 2:
+                    op("v", lambda: V.tensor_copy(o, i), rd, wr)
+                else:
+                    act(o, i, rd, wr)
+        gather(1)
+        cq, cs, lc, ls = T["ac%d" % t], T["as%d" % t], T["lc%d" % t], T["ls%d" % t]
+        quant(cq[:], cs[:], T.yt[:, 640:1280], [rg("yt", 640, 1280)], ["cq%d" % t])
+        dst = T.cores[rank ^ ROUNDS[t]]
+        rid, pid = topo.addr(dst)[0:2]
+        mask = 0
+        for e in topo.engines(core, dst)[0:8]:
+            mask |= 1 << e
+        wait("p", need([rg("cq%d" % t)], []))
+        arr, snt = T.sem["arr%d" % t], T.sem["snt%d" % t]
+        g.remote_dma(lc[:].bitcast(dt.uint8), cq[:].bitcast(dt.uint8), arr, snt, pid, rid, mask)
+        g.remote_dma(ls[:], cs[:], arr, snt, pid, rid, mask)
+        snap[("arr%d" % t, 16)] = {}
+        note(("arr%d" % t, 16), [], [rg("lc%d" % t)])
+        cnt["arr%d" % t] = cnt["snt%d" % t] = 16
+
+        gather(0)
+        quant(T.zq[:], T.zs[:], T.yt[:, 0:640], [rg("yt", 0, 640)], ["zq"])
+        for b in range(4):
+            act(T.y64[:, b:640:4], T.yt[:, b:640:4], [rg("yt", b, 640, 4)], [rg("y64", b, 640, 4)], 64.0)
+        for b in range(4):
+            k = bank()
+            w = (T.wq[:, 128 * b:128 * b + 128], T.wsc[:, 128 * b:128 * b + 128])
+            mm(k, 160, w, (T.zq[:], T.zs[:]), ["wq", "wsc", "zq"])
+            tt(T.t64[:, 160 * b:160 * b + 160], T["p%d" % k][:, 0:160], T.y64[:, b:640:4], A.add, ["p%d" % k, rg("y64", b, 640, 4)], [rg("t64", 160 * b, 160 * b + 160)])
+            act(T.xt[:, b:640:4], T.t64[:, 160 * b:160 * b + 160], [rg("t64", 160 * b, 160 * b + 160)], [rg("xt", b, 640, 4)], 0.015625)
+        quant_x(0)
+        if t < 2:
+            choose_half(0)
+        else:
+            mm(0, 160, (T.vq[:], T.vs[:]), xh(0), ["vq", rg("xq", 0, 160)])
+            ts(T.gi[:], T.w3[:], -160.0, 0.00078125, ["w3"], ["gi"], A.add, A.mult)
+            ts(T.n8[:], T.w3[:], 8.0, None, ["w3"], ["n8"], A.mult)
+            act(T.yo[:, 0:160], T.p0[:, 0:160], ["p0"], [rg("yo", 0, 160)])
+            ts(T.gt[:], T.gi[:], -10239.0, None, ["gi"], ["gt"], A.mult)
+            tt(T.nn[:, 0:20], T.n8[:], T.gt[:], A.add, ["n8", "gt"], ["nn"])
+            op("v", lambda: V.transpose(T.omt[:], T.nn[:]), ["nn"], ["omt"])
+        for b in range(4):
+            k = bank()
+            w = (T.wq[:, 128 * b:128 * b + 128], T.wsc[:, 128 * b:128 * b + 128])
+            e = EC * b
+            mm(k, 160, w, (lc[:], ls[:]), ["wq", "wsc", "lc%d" % t], True, False)
+            mm(k, 160, (T.eq[:, e:e + 128], T.es[:, e:e + 128]), (lc[:], ls[:]), ["eq", "lc%d" % t], False, True)
+            o, i = T.xt[:, 640 + b:1280:4], T["p%d" % k][:, 0:160]
+            rd, wr = ["p%d" % k], [rg("xt", 640 + b, 1280, 4)]
+            if t == 2 and b % 2 == 0:
+                ts(o, i, 0.015625, None, rd, wr, A.mult)
+            else:
+                act(o, i, rd, wr, 0.015625)
+        if t < 2:
+            unpack(0, 0, 160)
+        quant_x(1)
+        if t < 2:
+            choose_half(1)
+            unpack(0, 160, 320)
+            unpack(1, 0, 320)
+
+    def store_q(h, q1, q2):
+        lo, hi = 160 * h, 160 * h + 160
+        return [(q1, T.oc[:, 4 * lo:4 * hi], T.xq[:, lo:hi].bitcast(dt.uint8), [rg("xq", lo, hi)], [])] + \
+               [(q2, T.osc[4 * k:4 * k + 4, lo:hi], T.xs[32 * k:32 * k + 4, lo:hi], [rg("xq", lo, hi)], []) for k in range(4)]
+
+    jobs = [("s", T.om[c:c + 1, :], T.omt[32 * (c // 2):32 * (c // 2) + 20, 16 * (c % 2):16 * (c % 2) + 16], ["omt"], []) for c in range(8)]
+    jobs += store_q(0, "s", "s")
+    jobs += [("s", T.y[:, 0:160], T.yo[:, 0:160], [rg("yo", 0, 160)], [])]
+    mm(1, 160, (T.vq[:], T.vs[:]), xh(1), ["vq", rg("xq", 160, 320)])
+    op("v", lambda: V.tensor_copy(T.yo[:, 160:320], T.p1[:, 0:160]), ["p1"], [rg("yo", 160, 320)])
+    jobs += store_q(1, "s", "a")
+    jobs += [("s", T.y[:, 160:320], T.yo[:, 160:320], [rg("yo", 160, 320)], [])]
+    dmas("outs", jobs)
+    for s in SEMAPHORES:
+        if cnt.get(s, 0) > clock["p"].get(s, 0):
+            g.wait_ge(T.sem[s], cnt[s])

@@ -1,32 +1,48 @@
+import numpy as np
 from concourse.mybir import dt, AluOpType as A, ActivationFunctionType as AF
 
 ROUNDS = [1, 2, 4]
 BIG = float(2.0 ** 75)
-EC = 192
+FAR = 65536.0
+STEP = 5120.0
+EC = 208
 SCRATCH = {}
-for _d, _l in {"bfloat16": "xt 1280 yt 1280 y64 640 ut 512 vt 512 dg 192 et 3072 on 128 la 128 lb 128 lm 1024 hu 560 tw 10240",
-               "float32": "st 320 fm 320 rst 160 mk 96 zf 256 occ 8 fr 8 fb 8 wv 8 w0 8 val 320 win0 4096 win1 4096 win2 4096 "
-                          "w3 20 ng 20 sv 20 cc 2 gt 20 n8 20 nn 32 omt 32 yo 320 t64 640",
-               "int32": "pj 2 pk 2 gi 20", "uint16": "sl 20 gl 20"}.items():
-    _l = _l.split()
-    for _n, _w in zip(_l[::2], _l[1::2]):
-        SCRATCH[_n] = ("sbuf", [128, int(_w)], _d)
-for _n, _a, _b in (("hd", 2, 96), ("rr", 2, 96), ("sa", 2, 48), ("sb", 2, 24), ("am", 4, 96), ("am1", 4, 48), ("am2", 4, 24), ("am3", 4, 12),
-                   ("gb", 16, 12), ("gb1", 8, 12), ("gb2", 4, 12), ("wm", 8, 32), ("w1", 4, 20), ("w2", 2, 20)):
-    SCRATCH[_n] = ("sbuf", [128, _a, _b], "float32")
-for _n in "sc cb nc fp ff rj ac pa pb pc pd t0".split():
-    SCRATCH[_n] = ("sbuf", [128, 2, 12], "float32")
-for _n in "pi b0 b1 b2 b3 b4".split():
-    SCRATCH[_n] = ("sbuf", [128, 2, 12], "int32")
-for _n, _s, _w in [("xq", "xs", 320), ("uq", "us", 128), ("vq", "vs", 128), ("wq", "wsc", 512), ("eq", "es", 4 * EC), ("lq", "lqs", 256),
-                   ("hq", "hs", 140), ("zq", "zs", 160)] + [(_k + "c%d" % _t, _k + "s%d" % _t, 160) for _t in range(3) for _k in "al"]:
+
+
+def _declare(where, dtype, text):
+    for item in text.split():
+        name, dims = item.split(":")
+        SCRATCH[name] = (where, [128] + [int(k) for k in dims.split("x")], dtype)
+
+
+_declare("sbuf", "bfloat16", "xt:1280 yt:1280 y64:640 ut:512 vt:512 et:%d lm:1024 hu:768 tw:10240 gg:20x16 gs:10x9 h0:80 dd:160 "
+         "c320:160 mk9:180 mk8:80 mk4:320 val:320 va1:320 va2:320 win:2560 wt:2560" % (4 * EC + 8))
+_declare("sbuf", "float32", "st:320 fm:328 rst:160 pk:160 th:160 wv:8 z1:20 z2:20 z3:20 a1:80 rl:80 rs:160 occ:8 fb:8 rj:20 ac:20 fp:20 gb:180 gt:180 "
+         "s4:320 u1:80 w3:20 ng:20 sv:20 cc:2 pm:2 ul:8 n8:20 n1:20 n2:20 n3:20 nn:32 omt:32 yo:320 t64:640")
+_declare("sbuf", "int32", "pj:2 pq:2 pa:2 pb:2 gi:20 mi:20 m1:20")
+_declare("sbuf", "uint16", "sl:20 gl:20 uo:8")
+PAIRS = [("xq", "xs", 320), ("uq", "us", 128), ("u2", "u2s", 128), ("vq", "vs", 128), ("wq", "wsc", 512), ("eq", "es", 4 * EC), ("lq", "lqs", 256),
+         ("hq", "hs", 192), ("zq", "zs", 160)] + [(_k + "c%d" % _t, _k + "s%d" % _t, 160) for _t in range(3) for _k in "al"]
+for _n, _s, _w in PAIRS:
     SCRATCH[_n] = ("sbuf", [128, _w], "float8_e4m3fn_x4")
     SCRATCH[_s] = ("sbuf", [128, _w], "uint8")
+PLANE = {_n: _s for _n, _s, _w in PAIRS}
 for _t in range(8):
     SCRATCH["p%d" % _t] = ("psum", [128, 512], "float32")
-SEMAPHORES = ["qv", "qt", "qa", "qp", "dx0", "dx1", "du", "dv", "dw", "dz", "rota", "rotb", "lst", "outs",
-              "arr0", "arr1", "arr2", "snt0", "snt1", "snt2"]
-ALL = 1 << 20
+SEMAPHORES = ["qv", "qt", "qa", "qp", "dx0", "dx1", "du", "dv", "dw", "dl", "rot", "outs", "arr0", "arr1", "arr2", "snt0", "snt1", "snt2"]
+FEET = {}
+
+
+def _foot(name, idx):
+    key = (name, repr(idx))
+    if key not in FEET:
+        m = np.zeros(SCRATCH[name][1], bool)
+        m[idx] = True
+        m = m.reshape(128, -1)
+        if SCRATCH[name][0] == "psum":
+            m[:] = True
+        FEET[key] = (name,) + tuple(int.from_bytes(np.packbits(k).tobytes(), "big") for k in (m.any(axis=1), m.any(axis=0)))
+    return FEET[key]
 
 
 def rank_program(g, core, T, topo):
@@ -34,23 +50,30 @@ def rank_program(g, core, T, topo):
     if rank is None:
         return
     V, P, S, Y = g.vector, g.tensor, g.scalar, g.sync
+    s_ = np.s_
     queue = {"v": V, "t": P, "a": S, "s": Y, "p": g}
     own = {"v": "qv", "t": "qt", "a": "qa", "p": "qp"}
     cnt, clock, snap = {}, {q: {} for q in queue}, {}
-    wrote, read = {}, {}
+    wrote, read, pending = {}, {}, {}
 
-    def rg(name, lo=0, hi=ALL, step=1):
-        return (name, lo, hi, step)
+    def X(name, idx=s_[:]):
+        return (T[name][idx], [_foot(name, idx)])
+
+    def Q(name, lo, hi):
+        return X(name, s_[:, lo:hi]), X(PLANE[name], s_[:, lo:hi])
+
+    def by(win, off):
+        return (win[0].indirect(off[0]), win[1] + off[1])
 
     def meet(a, b):
-        if a[1] >= b[2] or b[1] >= a[2]:
-            return False
-        return not (a[3] == b[3] and a[3] > 1 and (a[1] - b[1]) % a[3] != 0)
+        return a[1] & b[1] and a[2] & b[2]
 
-    def need(rd, wr):
+    def need(q, rd, wr):
         d = []
         for r in rd:
             d += [t for (x, t) in wrote.get(r[0], []) if meet(r, x)]
+            if SCRATCH[r[0]][0] == "psum":
+                d += [t for (x, t) in read.get(r[0], []) if t[0] != own[q]]
         for r in wr:
             d += [t for (x, t) in wrote.get(r[0], []) + read.get(r[0], []) if meet(r, x)]
         return d
@@ -71,42 +94,50 @@ def rank_program(g, core, T, topo):
     def note(tok, rd, wr):
         for r in wr:
             for tab in (wrote, read):
-                tab[r[0]] = [(x, t) for (x, t) in tab.get(r[0], [])
-                             if not (r[1] <= x[1] and x[2] <= r[2] and (r[3] == 1 or (r[3] == x[3] and (r[1] - x[1]) % r[3] == 0)))]
+                tab[r[0]] = [(x, t) for (x, t) in tab.get(r[0], []) if x[1] & ~r[1] or x[2] & ~r[2]]
             wrote[r[0]].append((r, tok))
         for r in rd:
             read.setdefault(r[0], []).append((r, tok))
 
-    def norm(l):
-        return [rg(x) if isinstance(x, str) else x for x in l]
+    def feet(l):
+        return [f for x in l if isinstance(x, tuple) for f in x[1]]
 
-    def op(q, fn, rd, wr, free=()):
-        rd, wr, s = norm(rd), norm(wr), own[q]
+    def op(q, fn, rd, wr, adds=False):
+        rd, wr, s = feet(rd), feet(wr), own[q]
         n = cnt.get(s, 0)
-        wait(q, need(rd, [r for r in wr if r[0] not in free]) + ([(s, n)] if q == "p" and n else []))
+        wait(q, need(q, rd, [] if adds else wr) + ([(s, n)] if q == "p" and n else []))
         cnt[s] = n + 1
         tok = (s, n + 1)
         snap[tok] = dict(clock[q])
         fn().then_inc(T.sem[s], 1)
         note(tok, rd, wr)
 
-    def dmas(s, jobs):
-        cnt[s] = cnt.get(s, 0) + 16 * len(jobs)
-        tok, sn, done = (s, cnt[s]), None, []
-        for q, o, i, rd, wr in jobs:
-            rd, wr = norm(rd), norm(wr)
-            wait(q, need(rd, wr))
-            sn = dict(clock[q]) if sn is None else {k: min(v, sn.get(k, 0)) for k, v in clock[q].items()}
-            queue[q].dma_start(o, i).then_inc(T.sem[s], 16)
-            done.append((rd, wr))
-        snap[tok] = sn
-        for rd, wr in done:
-            note(tok, rd, wr)
+    def dmas(s, jobs, close=True):
+        for q, o, i in jobs:
+            wait(q, need(q, i[1], o[1]))
+            queue[q].dma_start(o[0], i[0]).then_inc(T.sem[s], 16)
+            pending.setdefault(s, []).append((dict(clock[q]), i[1], o[1]))
+        if close:
+            done = pending.pop(s)
+            cnt[s] = cnt.get(s, 0) + 16 * len(done)
+            tok = (s, cnt[s])
+            snap[tok] = {k: max(c.get(k, 0) for c, i, o in done) for c, i, o in done for k in c}
+            for c, i, o in done:
+                note(tok, i, o)
 
-    def mm(bank, n, lhs, rhs, rd, start=True, stop=True):
-        out = T["p%d" % bank][:, 0:n]
-        op("t", lambda: P.matmul_mx(out, lhs[0], lhs[1], rhs[0], rhs[1], start, stop), rd, ["p%d" % bank],
-           () if start else ("p%d" % bank,))
+    def hbm(ap):
+        return (ap, [])
+
+    def raw(x):
+        return (x[0].bitcast(dt.uint8), x[1])
+
+    def a_(x):
+        return x[0] if isinstance(x, tuple) else x
+
+    def mm(bank, n, lhs, rhs, start=True, stop=True):
+        out = X("p%d" % bank, s_[:, 0:n])
+        op("t", lambda: P.matmul_mx(out[0], lhs[0][0], lhs[1][0], rhs[0][0], rhs[1][0], start, stop), list(lhs + rhs), [out], not start)
+        return out
 
     pool = [0]
 
@@ -114,250 +145,267 @@ def rank_program(g, core, T, topo):
         pool[0] += 1
         return 2 + pool[0] % 6
 
-    def tt(o, a, b, k, rd, wr):
-        op("v", lambda: V.tensor_tensor(o, a, b, k), rd, wr)
+    def tt(o, a, b, k):
+        op("v", lambda: V.tensor_tensor(o[0], a[0], b[0], k), [a, b], [o])
 
-    def ts(o, a, s1, s2, rd, wr, k0, k1=None):
+    def ts(o, a, s1, k0, s2=None, k1=None):
         if k1 is None:
-            op("v", lambda: V.tensor_scalar(o, a, s1, None, k0), rd, wr)
+            op("v", lambda: V.tensor_scalar(o[0], a[0], a_(s1), None, k0), [a, s1], [o])
         else:
-            op("v", lambda: V.tensor_scalar(o, a, s1, s2, k0, k1), rd, wr)
+            op("v", lambda: V.tensor_scalar(o[0], a[0], a_(s1), a_(s2), k0, k1), [a, s1, s2], [o])
 
-    def act(o, i, rd, wr, scale=1.0):
-        op("a", lambda: S.activation(o, i, AF.Copy, scale=scale), rd, wr)
+    def scan(o, a, b, first, k0, k1):
+        op("v", lambda: V.tensor_tensor_scan(o[0], a[0], b[0], first, k0, k1), [a, b], [o])
 
-    def fill(ap, c, wr):
-        op("v", lambda: V.memset(ap, c), [], wr)
+    def copy(o, i):
+        op("v", lambda: V.tensor_copy(o[0], i[0]), [i], [o])
 
-    def quant(q, s, i, rd, wr):
-        op("v", lambda: V.quantize_mx(q, s, i), rd, wr)
+    def turn32(o, i):
+        op("v", lambda: V.transpose(o[0], i[0]), [i], [o])
 
-    dmas("dx0", [("s", T.xt[:, 0:640], T.x[:, 0:640], [], [rg("xt", 0, 640)])])
-    dmas("du", [("a", T.ut[:], T.u[:], [], ["ut"])])
-    dmas("dx1", [("s", T.xt[:, 640:1280], T.x[:, 640:1280], [], [rg("xt", 640, 1280)])])
+    def act(o, i, scale=None):
+        if scale is None:
+            op("a", lambda: S.activation(o[0], i[0], AF.Copy), [i], [o])
+        else:
+            op("a", lambda: S.activation(o[0], i[0], AF.Copy, scale=scale), [i], [o])
 
-    flag = {"allow_small_or_imprecise_dtypes": True}
-    quarters = [(a, slice(32 * a, 32 * a + 32)) for a in range(4)]
-    fill(T.dg[:], 0.0, ["dg"])
-    fill(T.on[:], 1.0, ["on"])
+    def fill(o, c):
+        op("v", lambda: V.memset(o[0], c), [], [o])
+
+    def quant(q, i):
+        op("v", lambda: V.quantize_mx(q[0][0], q[1][0], i[0]), [i], list(q))
+
+    def iota(o, pattern, base, step, whole=False):
+        if whole:
+            op("p", lambda: g.iota(o[0], pattern, base, step), [], [o])
+        else:
+            op("p", lambda: g.iota(o[0], pattern, base, step, allow_small_or_imprecise_dtypes=True), [], [o])
+
+    def select(o, pattern, k, c, base, step):
+        op("p", lambda: g.affine_select(o[0], o[0], pattern, k, c, base, step), [o], [o])
+
+    dmas("dx0", [("s", X("xt", s_[:, 0:640]), hbm(T.x[:, 0:640]))])
+    dmas("du", [("a", X("ut"), hbm(T.u[:]))])
+    dmas("dx1", [("s", X("xt", s_[:, 640:1280]), hbm(T.x[:, 640:1280]))])
+    dmas("dw", [("s", raw(X("wq")), hbm(T.wc[:])), ("s", X("wsc"), hbm(T.ws[:]))])
+    dmas("dv", [("s", X("vt"), hbm(T.v[:]))])
+
+    fill(X("hu"), 0.0)
+    fill(X("et"), 0.0)
+    iota(X("pq"), [[0, 2]], 7, 1, True)
+    iota(X("ul"), [[16, 8]], 0, 0)
+    for lo, hi in ((0, 128), (128, EC)):
+        select(X("et", s_[:, 4 * lo + 3:4 * hi:4]), [[-1, hi - lo]], A.not_equal, 64.0, 0, 1)
+    fill(X("lm"), 1.0)
+    for a in range(4):
+        select(X("lm", s_[32 * a:32 * a + 32, 0:512:4]), [[1, 4], [4, 32]], A.is_gt, 0.0, -a, -4)
+    for k in range(4):
+        act(X("win", s_[:, 640 * k:640 * k + 640]), X("hu", s_[:, 0:640]))
+    ts(X("pa"), X("pq"), 7, A.bitwise_and)
+    fill(X("rst"), 0.0)
+    copy(X("pm"), X("pa"))
+    fill(X("rst", s_[:, 0:160:16]), -BIG)
+    ts(X("uo"), X("ul"), X("pm", s_[:, 0:1]), A.add)
+    fill(X("fm", s_[:, 160:168]), 0.0)
+    fill(X("fm", s_[:, 320:328]), 0.0)
     for b in range(4):
-        fill(T.et[:, 4 * EC * b:4 * EC * (b + 1)], 0.0, [rg("et", 4 * EC * b, 4 * EC * (b + 1))])
-    fill(T.hu[:], 0.0, ["hu"])
-    for k in (0, 128):
-        op("p", lambda: g.affine_select(T.dg[:], T.dg[:], [[-1, EC]], A.not_equal, 64.0, k, 1), ["dg"], ["dg"])
-    for a, p in quarters:
-        op("p", lambda: g.affine_select(T.la[p, :], T.on[p, :], [[1, 4], [4, 32]], A.is_gt, 0.0, -a, -4), ["on"], [rg("la", a, a + 1)])
-    op("p", lambda: g.iota(T.zf[:], [[0, 256]], 0, 0, **flag), [], ["zf"])
-    op("p", lambda: g.affine_select(T.rst[:], T.zf[:, 0:160], [[0, 10], [1, 16]], A.not_equal, -BIG, 0, 0), ["zf"], ["rst"])
-    op("p", lambda: g.affine_select(T.mk[:], T.zf[:, 0:96], [[0, 8], [1, 12]], A.is_equal, 1.0, 0, 0), ["zf"], ["mk"])
-    for b in range(4):
-        act(T.et[:, 4 * EC * b + b:4 * EC * (b + 1):4], T.dg[:], ["dg"], [rg("et", 4 * EC * b + b, 4 * EC * (b + 1))])
-    for a, p in quarters:
-        op("p", lambda: g.iota(T.nc[p, :, :], [[32, 2], [8192, 12]], 64 * a + 1, 256, **flag), [], [rg("nc", a, a + 1)])
-    for a, p in quarters:
-        op("p", lambda: g.iota(T.val[p, :], [[1280, 2], [32, 10], [1, 16]], 2560 * a, 1, **flag), [], [rg("val", a, a + 1)])
-    op("p", lambda: g.iota(T.pj[:], [[0, 2]], 0, 1), [], ["pj"])
-    op("p", lambda: g.iota(T.nn[:], [[0, 32]], 0, 0, **flag), [], ["nn"])
-    dmas("dz", [("s", T["win%d" % t][0:128:16, :], T.zf[:], ["zf"], ["win%d" % t]) for t in range(3)])
-    dmas("dw", [("s", T.wq[:].bitcast(dt.uint8), T.wc[:], [], ["wq"]), ("s", T.wsc[:], T.ws[:], [], ["wsc"])])
-    dmas("dv", [("s", T.vt[:], T.v[:], [], ["vt"])])
+        quant(Q("eq", EC * b, EC * b + EC), X("et", s_[:, 3 - b:3 - b + 4 * EC]))
+    quant(Q("uq", 0, 128), X("ut"))
+    words = lambda x: (x[0].bitcast(dt.uint32), x[1])
+    copy(words(X("u2")), by(words(X("uq")), X("uo")))
+    act(X("u2s"), by(X("us"), X("uo")))
+    iota(X("val"), [[0, 4], [32, 5], [1, 16]], 0, 0)
+    iota(X("va1"), [[0, 4], [32, 5], [1, 16]], 16, 0)
+    iota(X("va2"), [[1280, 2], [640, 2], [0, 80]], 0, 80)
+    iota(X("pj"), [[0, 2]], 0, 1, True)
+    iota(X("nn"), [[0, 32]], 0, 0)
+    dmas("dl", [("s", X("val", s_[16:128:32, :]), X("va1", s_[0:4, :])), ("s", X("val", s_[8:128:32, :]), X("va2", s_[0:128:32, :])),
+                ("s", X("val", s_[24:128:32, :]), X("va2", s_[0:128:32, :]))])
 
-    U = (T.uq[:], T.us[:])
-    CC = T.cc[:, 0:1]
+    CC = X("cc", s_[:, 0:1])
 
     def xh(h):
-        return (T.xq[:, 160 * h:160 * h + 160], T.xs[:, 160 * h:160 * h + 160])
+        return Q("xq", 160 * h, 160 * h + 160)
 
     def quant_x(h):
+        quant(xh(h), X("xt", s_[:, 640 * h:640 * h + 640]))
+
+    def scores(h):
+        return mm(0, 160, Q("u2", 0, 128), xh(h))
+
+    def choose(h, p):
+        n, m = slice(10 * h, 10 * h + 10), slice(5 * h, 5 * h + 5)
         lo = 160 * h
-        quant(xh(h)[0], xh(h)[1], T.xt[:, 4 * lo:4 * lo + 640], [rg("xt", 4 * lo, 4 * lo + 640)], [rg("xq", lo, lo + 160)])
+        st, fm = X("st", s_[:, lo:lo + 160]), X("fm", s_[:, lo:lo + 160])
+        turn32(st, p)
+        scan(fm, st, X("rst"), 0.0, A.max, A.add)
+        tt(X("gg", s_[:, n, :]), fm, X("fm", s_[:, lo + 7:lo + 167]), A.is_ge)
+        tt(X("gs", s_[:, m, :]), X("gg", s_[:, 10 * h:10 * h + 10:2, 0:9]), X("gg", s_[:, 10 * h + 1:10 * h + 10:2, 0:9]), A.add)
+        for k in range(4):
+            o = 32 * (8 + 5 * h + k) + k
+            tt(X("hu", s_[:, o:o + 160:4]), X("gs", s_[:, m, 1:9]), X("gs", s_[:, m, 0:8]), A.subtract)
 
-    def choose_half(h):
-        lo, hi = 160 * h, 160 * h + 160
-        mm(0, 160, U, xh(h), ["uq", rg("xq", lo, hi)])
-        op("v", lambda: V.transpose(T.st[:, lo:hi], T.p0[:, 0:160]), ["p0"], [rg("st", lo, hi)])
-        op("v", lambda: V.tensor_tensor_scan(T.fm[:, lo:hi], T.rst[:], T.st[:, lo:hi], 0.0, A.add, A.max), ["rst", rg("st", lo, hi)], [rg("fm", lo, hi)])
-        for i in range(8):
-            o = 48 * (i + 1) + 20 * h
-            tt(T.hu[:, o:o + 20:2], T.fm[:, lo + i:hi:16], T.fm[:, lo + 7:hi:16], A.is_ge, [rg("fm", lo, hi)], [rg("hu", o, o + 20, 2)])
-
-    def unpack(d, lo, hi):
+    def unpack(d, h):
         for b in range(4):
-            k = bank()
-            e = EC * b + 16 * d
-            mm(k, hi - lo, (T.eq[:, e:e + 128], T.es[:, e:e + 128]), (T.xq[:, lo:hi], T.xs[:, lo:hi]), ["eq", rg("xq", lo, hi)])
-            o = 1280 * d + 320 * b
-            act(T.tw[:, o + lo:o + hi], T["p%d" % k][:, 0:hi - lo], ["p%d" % k], [rg("tw", o + lo, o + hi)], 0.015625)
+            e, o = EC * b + 16 * d, 1280 * d + 640 * h + 160 * b
+            act(X("tw", s_[:, o:o + 160]), mm(bank(), 160, Q("eq", e, e + 128), xh(h)), 0.015625)
 
-    def turn(s, d):
-        lo, hi = 1280 * d, 1280 * (d + 2)
-        dmas(s, [("s", T.tw[64 * k:64 * k + 64, 5120 + lo:5120 + hi], T.tw[64 - 64 * k:128 - 64 * k, lo:hi],
-                  [rg("tw", lo, hi)], [rg("tw", 5120 + lo, 5120 + hi)]) for k in range(2)])
+    def turn(ds, h, close=False):
+        jobs = []
+        for d in ds:
+            o = 1280 * d + 640 * h
+            jobs += [("s", X("tw", s_[64 * k:64 * k + 64, 5120 + o:5760 + o]), X("tw", s_[64 - 64 * k:128 - 64 * k, o:o + 640])) for k in range(2)]
+        dmas("rot", jobs, close)
 
-    for b in range(4):
-        e = EC * b
-        quant(T.eq[:, e:e + EC], T.es[:, e:e + EC], T.et[:, 4 * e:4 * e + 4 * EC], [rg("et", 4 * e, 4 * e + 4 * EC)], [rg("eq", e, e + EC)])
-    ts(T.lb[:], T.la[:], -1.0, 1.0, ["la"], ["lb"], A.mult, A.add)
-    quant(T.uq[:], T.us[:], T.ut[:], ["ut"], ["uq"])
     quant_x(0)
+    p = scores(0)
+    quant(Q("hq", 0, 128), X("hu", s_[:, 0:512]))
+    choose(0, p)
+    unpack(0, 0)
     quant_x(1)
-    for t in (0, 2, 1, 3):
-        for k in range(2):
-            src = "lb" if t % 2 else "la"
-            act(T.lm[:, 512 * k + t:512 * k + 512:4], T[src][:], [src], [rg("lm", 512 * k + t, 512 * k + 512, 4)], -1.0 if k else 1.0)
-    choose_half(0)
-    choose_half(1)
-    quant(T.lq[:], T.lqs[:], T.lm[:], ["lm"], ["lq"])
-    unpack(0, 0, 320)
-    unpack(1, 0, 320)
 
     for t in range(3):
-        W = T["win%d" % t]
-        op("v", lambda: V.tensor_copy(T.hu[:, 5:432:2], T.hu[:, 0:427:2]), [rg("hu", 0, 432, 2)], [rg("hu", 5, 433, 2)])
-        quant(T.hq[:], T.hs[:], T.hu[:], ["hu"], ["hq"])
-        mm(1, 128, (T.lq[:, 0:128], T.lqs[:, 0:128]), (T.hq[:, 12:140], T.hs[:, 12:140]), ["lq", "hq"], True, False)
-        mm(1, 128, (T.lq[:, 128:256], T.lqs[:, 128:256]), (T.hq[:, 0:128], T.hs[:, 0:128]), ["lq", "hq"], False, True)
-        for e in range(2):
-            tt(T.hd[:, e, :], T.hu[:, 48 + 2 * e:432:4], T.hu[:, 2 * e:384:4], A.subtract, [rg("hu", 0, 432, 2)], ["hd%d" % e])
-        for e in range(2):
-            tt(T.sa[:, e, :], T.hu[:, 48 + 2 * e:240:4], T.hu[:, 240 + 2 * e:432:4], A.add, [rg("hu", 0, 432, 2)], ["sa%d" % e])
-        tt(T.sb[:], T.sa[:, :, 0:24], T.sa[:, :, 24:48], A.add, ["sa0", "sa1"], ["sb"])
-        tt(T.sc[:], T.sb[:, :, 0:12], T.sb[:, :, 12:24], A.add, ["sb"], ["sc"])
-        ts(T.cb[:], T.sc[:], -16384.0, 131072.0, ["sc"], ["cb"], A.mult, A.add)
-        op("v", lambda: V.tensor_tensor_scan(T.rr[:, 0, :], T.mk[:], T.p1[:, 0:96], 0.0, A.mult, A.add), ["mk", "p1"], ["rr0"])
-        tt(T.rr[:, 1, :], T.rr[:, 0, :], T.hd[:, 0, :], A.add, ["rr0", "hd0"], ["rr1"])
-        for e in range(2):
-            tt(T.am[:, e, :], T.rr[:, e, :], T.hd[:, e, :], A.mult, ["rr%d" % e, "hd%d" % e], ["am%d" % e])
-            ts(T.am[:, 2 + e, :], T.rr[:, e, :], 320.0, 32.0, ["rr%d" % e], ["am%d" % (2 + e)], A.min, A.mult)
-        ts(T.occ[:], T.rr[:, 0, 10:96:12], 320.0, None, ["rr0"], ["occ"], A.min)
-        tt(T.am1[:], T.am[:, :, 0:48], T.am[:, :, 48:96], A.add, ["am0", "am1", "am2", "am3"], ["am_1"])
-        ts(T.fr[:], T.occ[:], -32.0, 10240.0, ["occ"], ["fr"], A.mult, A.add)
-        ts(T.wv[:], T.occ[:], 32.0, 6144.0, ["occ"], ["wv"], A.mult, A.add)
-        ts(T.w0[:], T.occ[:], 32.0, -1.0, ["occ"], ["w0"], A.mult, A.add)
-        tt(T.am2[:], T.am1[:, :, 0:24], T.am1[:, :, 24:48], A.add, ["am_1"], ["am_2"])
-        op("v", lambda: V.tensor_tensor_scan(T.fb[:], T.fr[:], T.zf[:, 0:8], 1.0, A.add, A.add), ["fr", "zf"], ["fb"])
-        tt(T.am3[:], T.am2[:, :, 0:12], T.am2[:, :, 12:24], A.add, ["am_2"], ["am_3"])
-        CS, MS = T.am3[:, 0:2, :], T.am3[:, 2:4, :]
-        tt(T.fp[:], T.nc[:], MS, A.subtract, ["nc", "am_3"], ["fp"])
-        ts(T.rj[:], CS, 320.0, None, ["am_3"], ["rj"], A.is_ge)
-        ts(T.pa[:], CS, 32.0, None, ["am_3"], ["pa"], A.mult)
-        ts(T.ac[:], CS, 320.0, None, ["am_3"], ["ac"], A.is_lt)
-        tt(T.ff[:], T.fp[:], T.rj[:], A.mult, ["fp", "rj"], ["ff"])
-        tt(T.pb[:], T.pa[:], T.cb[:], A.add, ["pa", "cb"], ["pb"])
-        ts(T.t0[:], T.rj[:], T.w0[:, 0:1], None, ["rj", "w0"], ["t0"], A.mult)
-        for c in range(1, 8):
-            ts(T.gb[:, 2 * c:2 * c + 2, :], T.ff[:], T.fb[:, c - 1:c], T.wv[:, c:c + 1], ["ff", "fb", "wv"], ["gb%d" % c], A.is_ge, A.mult)
-            if c == 2:
-                tt(T.pc[:], T.pb[:], T.ac[:], A.mult, ["pb", "ac"], ["pc"])
-            if c == 4:
-                tt(T.pd[:], T.pc[:], T.t0[:], A.add, ["pc", "t0"], ["pd"])
-            if c == 6:
-                tt(T.gb[:, 0:2, :], T.ff[:], T.pd[:], A.add, ["ff", "pd"], ["gb0"])
-        tt(T.gb1[:], T.gb[:, 0:8, :], T.gb[:, 8:16, :], A.add, ["gb%d" % c for c in range(8)], ["gb_1"])
-        tt(T.gb2[:], T.gb1[:, 0:4, :], T.gb1[:, 4:8, :], A.add, ["gb_1"], ["gb_2"])
-        tt(T.pi[:], T.gb2[:, 0:2, :], T.gb2[:, 2:4, :], A.add, ["gb_2"], ["pi"])
-        ts(T.b0[:], T.pi[:], 480, None, ["pi"], ["b0"], A.bitwise_and)
-        ts(T.b1[:], T.pi[:], 5, 3584, ["pi"], ["b1"], A.arith_shift_right, A.bitwise_and)
-        ts(T.b2[:], T.pi[:], 9, 31, ["pi"], ["b2"], A.arith_shift_right, A.bitwise_and)
-        tt(T.b3[:], T.b0[:], T.b1[:], A.add, ["b0", "b1"], ["b3"])
-        tt(T.b4[:], T.b3[:], T.b2[:], A.add, ["b3", "b2"], ["b4"])
-        for e in range(2):
-            op("v", lambda: V.tensor_copy(T.sl[:, 10 * e:10 * e + 10], T.b4[:, e, 0:10]), ["b4"], [rg("sl", 10 * e, 10 * e + 10)])
-        op("v", lambda: V.tensor_copy(W[:].indirect(T.sl[:]), T.val[:]), ["sl", "val"], ["win%d" % t])
-        turn("rota", 0)
-        unpack(2, 0, 320)
-        unpack(3, 0, 320)
-        turn("rotb", 2)
-        dmas("lst", [("as"[x % 2], T.wm[:, x, :], W[16 * x:16 * x + 1, :], ["win%d" % t], ["wm%d" % x]) for x in range(8)])
+        p = scores(1)
         if t == 0:
-            quant(T.vq[:], T.vs[:], T.vt[:], ["vt"], ["vq"])
-            ts(T.pk[:], T.pj[:], 4, None, ["pj"], ["pk"], A.arith_shift_right)
-            ts(T.cc[:], T.pk[:], 1280.0, None, ["pk"], ["cc"], A.mult)
-        tt(T.w1[:], T.wm[:, 0:4, 0:20], T.wm[:, 4:8, 0:20], A.add, ["wm%d" % x for x in range(8)], ["w1"])
-        tt(T.w2[:], T.w1[:, 0:2, :], T.w1[:, 2:4, :], A.add, ["w1"], ["w2"])
-        tt(T.w3[:], T.w2[:, 0, :], T.w2[:, 1, :], A.add, ["w2"], ["w3"])
-        ts(T.ng[:], T.w3[:], CC, 10240.0, ["w3", "cc"], ["ng"], A.is_lt, A.mult)
-        tt(T.sv[:], T.w3[:], T.ng[:], A.add, ["w3", "ng"], ["sv"])
-        ts(T.gl[:], T.sv[:], CC, None, ["sv", "cc"], ["gl"], A.subtract)
+            quant(Q("lq", 0, 256), X("lm"))
+        unpack(1, 0)
+        turn((0, 1), 0)
+        unpack(2, 1)
+        choose(1, p)
+        quant(Q("hq", 64, 192), X("hu", s_[:, 256:768]))
+        for k in range(3):
+            mm(1, 128, Q("lq", 128 * min(k, 1), 128 * min(k, 1) + 128), Q("hq", 64 - 32 * k, 192 - 32 * k), k == 0, k == 2)
+        unpack(3, 1)
+        turn((2, 3), 1)
+        unpack(2, 0)
+        unpack(3, 0)
+        turn((2, 3), 0, True)
+        for d in (0, 1, 4, 5):
+            unpack(d, 1)
+        if t == 0:
+            for name, n in (("mk8", 8), ("mk9", 9), ("mk4", 4)):
+                fill(X(name), 1.0)
+                fill(X(name, s_[:, 0::n]), 0.0)
+            fill(X("c320"), 320.0)
+        A0 = X("p1", s_[:, 0:80])
+        for e in range(2):
+            ts(X("dd", s_[:, 80 * e:80 * e + 80]), X("gg", s_[:, e:20:2, 0:8]), -STEP - FAR, A.mult, FAR, A.add)
+        tt(X("h0"), X("gg", s_[:, 0:20:2, 1:9]), X("gg", s_[:, 0:20:2, 0:8]), A.subtract)
+        scan(X("th"), X("dd"), X("c320"), 0.0, A.add, A.min)
+        tt(X("a1"), A0, X("h0"), A.add)
+        ts(X("rl"), A0, 320.0, A.max, 8.5 / 8 - 320.0, A.add)
+        scan(X("pk", s_[:, 0:80]), X("dd", s_[:, 0:80]), A0, 0.0, A.add, A.min)
+        ts(X("occ"), X("p1", s_[:, 80:88]), 320.0, A.min)
+        scan(X("pk", s_[:, 80:160]), X("dd", s_[:, 80:160]), X("a1"), 0.0, A.add, A.min)
+        scan(X("rs", s_[:, 0:80]), X("mk8"), X("rl"), 0.0, A.mult, A.add)
+        scan(X("fb"), X("c320", s_[:, 0:8]), X("occ"), 8.5, A.add, A.subtract)
+        F, TH, O0 = X("pk", s_[:, 7:160:8]), X("th", s_[:, 7:160:8]), X("occ", s_[:, 0:1])
+        tt(X("rj"), F, TH, A.is_ge)
+        tt(X("ac"), F, TH, A.is_lt)
+        ts(X("fp"), F, 7 * STEP + 8.5, A.add, O0, A.subtract)
+        ts(X("wv"), X("occ"), STEP - 320.0, A.add)
+        tt(X("rs", s_[:, 87:160:8]), X("rs", s_[:, 7:80:8]), X("rj", s_[:, 0:10]), A.add)
+        tt(X("gb", s_[:, 1:180:9]), X("fp"), X("ac"), A.mult)
+        FF = X("gb", s_[:, 0:180:9])
+        tt(FF, X("rs", s_[:, 7:160:8]), X("rj"), A.mult)
+        for c in range(1, 8):
+            ts(X("gb", s_[:, c + 1:180:9]), FF, X("fb", s_[:, c - 1:c]), A.is_ge, X("wv", s_[:, c:c + 1]), A.mult)
+        scan(X("gt"), X("mk9"), X("gb"), 0.0, A.mult, A.add)
+        GT = X("gt", s_[:, 8:180:9])
+        ts(X("m1"), GT, O0, A.add, 0.0625, A.mult)
+        ts(X("z1"), GT, O0, A.add, 20.0, A.mult)
+        ts(X("z2"), X("m1"), -319.0, A.mult, 149.0, A.add)
+        tt(X("z3"), X("z1"), X("z2"), A.add)
+        copy(X("sl"), X("z3"))
+        op("v", lambda: V.tensor_copy(T.win[:].indirect(T.sl[:]), T.val[:]), [X("sl"), X("val")], [X("win")])
+        for k in range(20):
+            turn32(X("wt", s_[:, 128 * k:128 * k + 128]), X("win", s_[:, k:2560:20]))
+        if t == 0:
+            ts(X("pb"), X("pj"), 4, A.arith_shift_right)
+        scan(X("s4"), X("mk4"), X("wt", s_[:, 0:2560:8]), 0.0, A.mult, A.add)
+        if t == 0:
+            ts(X("cc"), X("pb"), 1280.0, A.mult)
+        tt(X("u1", s_[0:64]), X("s4", s_[0:64, 3:320:4]), X("s4", s_[64:128, 3:320:4]), A.add)
+        for a in range(4):
+            tt(X("w3", s_[32 * a:32 * a + 32]), X("u1", s_[0:32, a:80:4]), X("u1", s_[32:64, a:80:4]), A.add)
+        ts(X("ng"), X("w3"), CC, A.is_lt, 10240.0, A.mult)
+        tt(X("sv"), X("w3"), X("ng"), A.add)
+        ts(X("gl"), X("sv"), CC, A.subtract)
 
         def gather(h):
             for b in (0, 2, 1, 3):
-                o = T.yt[:, 640 * h + b:640 * h + 640:4]
-                i = T.tw[:, 320 * b:320 * b + 9280].indirect(T.gl[:, 10 * h:10 * h + 10])
-                rd, wr = ["gl", rg("tw", 320 * b, 320 * b + 9280)], [rg("yt", 640 * h + b, 640 * h + 640, 4)]
+                o = X("yt", s_[:, 640 * h + b:640 * h + 640:4])
+                i = by(X("tw", s_[:, 160 * b:160 * b + 9760]), X("gl", s_[:, 10 * h:10 * h + 10]))
                 if b < 2:
-                    op("v", lambda: V.tensor_copy(o, i), rd, wr)
+                    copy(o, i)
                 else:
-                    act(o, i, rd, wr)
+                    act(o, i)
         gather(1)
-        cq, cs, lc, ls = T["ac%d" % t], T["as%d" % t], T["lc%d" % t], T["ls%d" % t]
-        quant(cq[:], cs[:], T.yt[:, 640:1280], [rg("yt", 640, 1280)], ["cq%d" % t])
+        out, land = Q("ac%d" % t, 0, 160), Q("lc%d" % t, 0, 160)
+        quant(out, X("yt", s_[:, 640:1280]))
         dst = T.cores[rank ^ ROUNDS[t]]
         rid, pid = topo.addr(dst)[0:2]
         mask = 0
         for e in topo.engines(core, dst)[0:8]:
             mask |= 1 << e
-        wait("p", need([rg("cq%d" % t)], []))
+        wait("p", need("p", feet(out), []))
         arr, snt = T.sem["arr%d" % t], T.sem["snt%d" % t]
-        g.remote_dma(lc[:].bitcast(dt.uint8), cq[:].bitcast(dt.uint8), arr, snt, pid, rid, mask)
-        g.remote_dma(ls[:], cs[:], arr, snt, pid, rid, mask)
+        g.remote_dma(raw(land[0])[0], raw(out[0])[0], arr, snt, pid, rid, mask)
+        g.remote_dma(land[1][0], out[1][0], arr, snt, pid, rid, mask)
         snap[("arr%d" % t, 16)] = {}
-        note(("arr%d" % t, 16), [], [rg("lc%d" % t)])
+        note(("arr%d" % t, 16), [], feet(land))
         cnt["arr%d" % t] = cnt["snt%d" % t] = 16
+        if t < 2:
+            iota(X("win"), [[0, 2560]], 0, 0)
 
         gather(0)
-        quant(T.zq[:], T.zs[:], T.yt[:, 0:640], [rg("yt", 0, 640)], ["zq"])
-        for b in range(4):
-            act(T.y64[:, b:640:4], T.yt[:, b:640:4], [rg("yt", b, 640, 4)], [rg("y64", b, 640, 4)], 64.0)
-        for b in range(4):
-            k = bank()
-            w = (T.wq[:, 128 * b:128 * b + 128], T.wsc[:, 128 * b:128 * b + 128])
-            mm(k, 160, w, (T.zq[:], T.zs[:]), ["wq", "wsc", "zq"])
-            tt(T.t64[:, 160 * b:160 * b + 160], T["p%d" % k][:, 0:160], T.y64[:, b:640:4], A.add, ["p%d" % k, rg("y64", b, 640, 4)], [rg("t64", 160 * b, 160 * b + 160)])
-            act(T.xt[:, b:640:4], T.t64[:, 160 * b:160 * b + 160], [rg("t64", 160 * b, 160 * b + 160)], [rg("xt", b, 640, 4)], 0.015625)
+        quant(Q("zq", 0, 160), X("yt", s_[:, 0:640]))
+        for b in (2, 3, 0, 1):
+            act(X("y64", s_[:, b:640:4]), X("yt", s_[:, b:640:4]), 64.0)
+        for b in (2, 3, 0, 1):
+            p = mm(bank(), 160, Q("wq", 128 * b, 128 * b + 128), Q("zq", 0, 160))
+            tt(X("t64", s_[:, 160 * b:160 * b + 160]), p, X("y64", s_[:, b:640:4]), A.add)
+            act(X("xt", s_[:, b:640:4]), X("t64", s_[:, 160 * b:160 * b + 160]), 0.015625)
+        if t == 1:
+            quant(Q("vq", 0, 128), X("vt"))
         quant_x(0)
         if t < 2:
-            choose_half(0)
+            choose(0, scores(0))
         else:
-            mm(0, 160, (T.vq[:], T.vs[:]), xh(0), ["vq", rg("xq", 0, 160)])
-            ts(T.gi[:], T.w3[:], -160.0, 0.00078125, ["w3"], ["gi"], A.add, A.mult)
-            ts(T.n8[:], T.w3[:], 8.0, None, ["w3"], ["n8"], A.mult)
-            act(T.yo[:, 0:160], T.p0[:, 0:160], ["p0"], [rg("yo", 0, 160)])
-            ts(T.gt[:], T.gi[:], -10239.0, None, ["gi"], ["gt"], A.mult)
-            tt(T.nn[:, 0:20], T.n8[:], T.gt[:], A.add, ["n8", "gt"], ["nn"])
-            op("v", lambda: V.transpose(T.omt[:], T.nn[:]), ["nn"], ["omt"])
+            p = mm(0, 160, Q("vq", 0, 128), xh(0))
+            ts(X("gi"), X("w3"), -400.0, A.add, 0.00078125, A.mult)
+            ts(X("mi"), X("w3"), -80.0, A.add, 0.0015625, A.mult)
+            ts(X("n8"), X("w3"), 8.0, A.mult)
+            act(X("yo", s_[:, 0:160]), p)
+            ts(X("n1"), X("gi"), -2559.0, A.mult)
+            ts(X("n2"), X("mi"), -3840.0, A.mult)
+            tt(X("n3"), X("n8"), X("n1"), A.add)
+            tt(X("nn", s_[:, 0:20]), X("n3"), X("n2"), A.add)
+            turn32(X("omt"), X("nn"))
         for b in range(4):
             k = bank()
-            w = (T.wq[:, 128 * b:128 * b + 128], T.wsc[:, 128 * b:128 * b + 128])
-            e = EC * b
-            mm(k, 160, w, (lc[:], ls[:]), ["wq", "wsc", "lc%d" % t], True, False)
-            mm(k, 160, (T.eq[:, e:e + 128], T.es[:, e:e + 128]), (lc[:], ls[:]), ["eq", "lc%d" % t], False, True)
-            o, i = T.xt[:, 640 + b:1280:4], T["p%d" % k][:, 0:160]
-            rd, wr = ["p%d" % k], [rg("xt", 640 + b, 1280, 4)]
+            mm(k, 160, Q("wq", 128 * b, 128 * b + 128), land, True, False)
+            p = mm(k, 160, Q("eq", EC * b, EC * b + 128), land, False, True)
+            o = X("xt", s_[:, 640 + b:1280:4])
             if t == 2 and b % 2 == 0:
-                ts(o, i, 0.015625, None, rd, wr, A.mult)
+                ts(o, p, 0.015625, A.mult)
             else:
-                act(o, i, rd, wr, 0.015625)
+                act(o, p, 0.015625)
         if t < 2:
-            unpack(0, 0, 160)
+            unpack(0, 0)
         quant_x(1)
-        if t < 2:
-            choose_half(1)
-            unpack(0, 160, 320)
-            unpack(1, 0, 320)
 
     def store_q(h, q1, q2):
         lo, hi = 160 * h, 160 * h + 160
-        return [(q1, T.oc[:, 4 * lo:4 * hi], T.xq[:, lo:hi].bitcast(dt.uint8), [rg("xq", lo, hi)], [])] + \
-               [(q2, T.osc[4 * k:4 * k + 4, lo:hi], T.xs[32 * k:32 * k + 4, lo:hi], [rg("xq", lo, hi)], []) for k in range(4)]
+        return [(q1, hbm(T.oc[:, 4 * lo:4 * hi]), raw(X("xq", s_[:, lo:hi])))] + \
+               [(q2, hbm(T.osc[4 * k:4 * k + 4, lo:hi]), X("xs", s_[32 * k:32 * k + 4, lo:hi])) for k in range(4)]
 
-    jobs = [("s", T.om[c:c + 1, :], T.omt[32 * (c // 2):32 * (c // 2) + 20, 16 * (c % 2):16 * (c % 2) + 16], ["omt"], []) for c in range(8)]
-    jobs += store_q(0, "s", "s")
-    jobs += [("s", T.y[:, 0:160], T.yo[:, 0:160], [rg("yo", 0, 160)], [])]
-    mm(1, 160, (T.vq[:], T.vs[:]), xh(1), ["vq", rg("xq", 160, 320)])
-    op("v", lambda: V.tensor_copy(T.yo[:, 160:320], T.p1[:, 0:160]), ["p1"], [rg("yo", 160, 320)])
+    jobs = store_q(0, "s", "s")
+    jobs += [("s", hbm(T.y[:, 0:160]), X("yo", s_[:, 0:160]))]
+    jobs += [("s", hbm(T.om[c:c + 1, :]), X("omt", s_[32 * (c // 2):32 * (c // 2) + 20, 16 * (c % 2):16 * (c % 2) + 16])) for c in range(8)]
+    copy(X("yo", s_[:, 160:320]), mm(1, 160, Q("vq", 0, 128), xh(1)))
     jobs += store_q(1, "s", "a")
-    jobs += [("s", T.y[:, 160:320], T.yo[:, 160:320], [rg("yo", 160, 320)], [])]
+    jobs += [("s", hbm(T.y[:, 160:320]), X("yo", s_[:, 160:320]))]
     dmas("outs", jobs)
     for s in SEMAPHORES:
         if cnt.get(s, 0) > clock["p"].get(s, 0):

@@ -5,8 +5,10 @@ ROUNDS = [1, 2, 4]
 BIG = float(2.0 ** 75)
 FAR = 65536.0
 STEP = 5120.0
+WHOLE = 12582912.0
 EC = 208
 SCRATCH = {}
+OPT = {"rfirst": (1,),  "pe": (0, 1, 4, 5)}
 
 
 def _declare(where, dtype, text):
@@ -15,11 +17,11 @@ def _declare(where, dtype, text):
         SCRATCH[name] = (where, [128] + [int(k) for k in dims.split("x")], dtype)
 
 
-_declare("sbuf", "bfloat16", "xt:1280 yt:1280 y64:640 ut:512 vt:512 et:%d lm:1024 hu:768 tw:10240 gg:20x16 gs:10x9 h0:80 dd:160 "
-         "c320:160 mk9:180 mk8:80 mk4:320 val:320 va1:320 va2:320 win:2560 wt:2560" % (4 * EC + 8))
-_declare("sbuf", "float32", "st:320 fm:328 rst:160 pk:160 th:160 wv:8 z1:20 z2:20 z3:20 a1:80 rl:80 rs:160 occ:8 fb:8 rj:20 ac:20 fp:20 gb:180 gt:180 "
-         "s4:320 u1:80 w3:20 ng:20 sv:20 cc:2 pm:2 ul:8 n8:20 n1:20 n2:20 n3:20 nn:32 omt:32 yo:320 t64:640")
-_declare("sbuf", "int32", "pj:2 pq:2 pa:2 pb:2 gi:20 mi:20 m1:20")
+_declare("sbuf", "bfloat16", "xt:1280 yt:1280 y64:640 ut:512 vt:512 et:%d lm:1024 hu:768 tw:11520 gg:20x16 gs:10x9 h0:80 dd:160 "
+         "c320:160 mk8:160 mk4:160 val:320 va1:320 va2:320 win:2560 win0:2560 wt:2560" % (4 * EC + 8))
+_declare("sbuf", "float32", "st:320 fm:336 rst:160 pk:160 th:160 wv:8 z3:20 a1:80 rl:160 rs:160 occ:8 fb:8 ac:20 fp:20 gb:240 gt:240 mg:240 "
+         "s4:320 u1:80 w3:20 cc:1 pm:1 ph:1 ul:8 tb:8 tc:8 td:8 te:8 n1:20 n2:20 n3:20 n4:20 n5:20 n6:20 nn:32 omt:32 yo:320 t64:640")
+_declare("sbuf", "int32", "pa:1 pb:1 pc:1 pd:1 ti:16 tj:8 gi:20 mi:20 gj:20 gk:20")
 _declare("sbuf", "uint16", "sl:20 gl:20 uo:8")
 PAIRS = [("xq", "xs", 320), ("uq", "us", 128), ("u2", "u2s", 128), ("vq", "vs", 128), ("wq", "wsc", 512), ("eq", "es", 4 * EC), ("lq", "lqs", 256),
          ("hq", "hs", 192), ("zq", "zs", 160)] + [(_k + "c%d" % _t, _k + "s%d" % _t, 160) for _t in range(3) for _k in "al"]
@@ -29,7 +31,7 @@ for _n, _s, _w in PAIRS:
 PLANE = {_n: _s for _n, _s, _w in PAIRS}
 for _t in range(8):
     SCRATCH["p%d" % _t] = ("psum", [128, 512], "float32")
-SEMAPHORES = ["qv", "qt", "qa", "qp", "dx0", "dx1", "du", "dv", "dw", "dl", "rot", "outs", "arr0", "arr1", "arr2", "snt0", "snt1", "snt2"]
+SEMAPHORES = ["qv", "qt", "qa", "qp", "dx0", "dx1", "du", "dv", "dw", "dl", "dz", "rot", "outs", "arr0", "arr1", "arr2", "snt0", "snt1", "snt2"]
 FEET = {}
 
 
@@ -102,12 +104,16 @@ def rank_program(g, core, T, topo):
     def feet(l):
         return [f for x in l if isinstance(x, tuple) for f in x[1]]
 
-    def op(q, fn, rd, wr, adds=False):
+    across = []
+
+    def op(q, fn, rd, wr, adds=False, kind=None):
         rd, wr, s = feet(rd), feet(wr), own[q]
         n = cnt.get(s, 0)
-        wait(q, need(q, rd, [] if adds else wr) + ([(s, n)] if q == "p" and n else []))
+        wait(q, need(q, rd, [] if adds else wr) + ([(s, n)] if q == "p" and n else []) + (across[-1:] if q == "v" and not kind else []))
         cnt[s] = n + 1
         tok = (s, n + 1)
+        if kind == "across":
+            across.append(tok)
         snap[tok] = dict(clock[q])
         fn().then_inc(T.sem[s], 1)
         note(tok, rd, wr)
@@ -124,6 +130,13 @@ def rank_program(g, core, T, topo):
             snap[tok] = {k: max(c.get(k, 0) for c, i, o in done) for c, i, o in done for k in c}
             for c, i, o in done:
                 note(tok, i, o)
+
+    def weave(*chains):
+        chains = list(chains)
+        while chains:
+            for c in list(chains):
+                if next(c, "end") == "end":
+                    chains.remove(c)
 
     def hbm(ap):
         return (ap, [])
@@ -143,10 +156,10 @@ def rank_program(g, core, T, topo):
 
     def bank():
         pool[0] += 1
-        return 2 + pool[0] % 6
+        return 3 + pool[0] % 5
 
     def tt(o, a, b, k):
-        op("v", lambda: V.tensor_tensor(o[0], a[0], b[0], k), [a, b], [o])
+        op("v", lambda: V.tensor_tensor(o[0], a[0], b[0], k), [a, b], [o], kind="across" if a[1][0][1] != b[1][0][1] else None)
 
     def ts(o, a, s1, k0, s2=None, k1=None):
         if k1 is None:
@@ -161,10 +174,12 @@ def rank_program(g, core, T, topo):
         op("v", lambda: V.tensor_copy(o[0], i[0]), [i], [o])
 
     def turn32(o, i):
-        op("v", lambda: V.transpose(o[0], i[0]), [i], [o])
+        op("v", lambda: V.transpose(o[0], i[0]), [i], [o], kind="turn")
 
-    def act(o, i, scale=None):
-        if scale is None:
+    def act(o, i, scale=None, bias=None):
+        if bias is not None:
+            op("a", lambda: S.activation(o[0], i[0], AF.Identity, bias=bias[0], scale=0.0), [i, bias], [o])
+        elif scale is None:
             op("a", lambda: S.activation(o[0], i[0], AF.Copy), [i], [o])
         else:
             op("a", lambda: S.activation(o[0], i[0], AF.Copy, scale=scale), [i], [o])
@@ -190,157 +205,188 @@ def rank_program(g, core, T, topo):
     dmas("dw", [("s", raw(X("wq")), hbm(T.wc[:])), ("s", X("wsc"), hbm(T.ws[:]))])
     dmas("dv", [("s", X("vt"), hbm(T.v[:]))])
 
-    fill(X("hu"), 0.0)
     fill(X("et"), 0.0)
-    iota(X("pq"), [[0, 2]], 7, 1, True)
+    iota(X("ti"), [[-32, 4], [0, 2], [7, 2]], 128, 1, True)
+    iota(X("tb"), [[0, 4], [1280, 2]], -1280, 0)
     iota(X("ul"), [[16, 8]], 0, 0)
     for lo, hi in ((0, 128), (128, EC)):
         select(X("et", s_[:, 4 * lo + 3:4 * hi:4]), [[-1, hi - lo]], A.not_equal, 64.0, 0, 1)
     fill(X("lm"), 1.0)
+    ts(X("tj"), X("ti", s_[:, 0:16:2]), 5, A.arith_shift_right, 3, A.bitwise_and)
+    ts(X("pc"), X("ti", s_[:, 0:1]), 3, A.arith_shift_right, 1, A.bitwise_and)
+    ts(X("pa"), X("ti", s_[:, 1:2]), 7, A.bitwise_and)
+    fill(X("hu"), 0.0)
+    ts(X("tc"), X("tj"), -2560.0, A.mult)
+    copy(X("ph"), X("pc"))
+    copy(X("pm"), X("pa"))
+    fill(X("rst"), 0.0)
+    tt(X("td"), X("tc"), X("tb"), A.add)
+    ts(X("uo"), X("ul"), X("pm"), A.add)
+    fill(X("fm", s_[:, 160:168]), 0.0)
+    fill(X("fm", s_[:, 328:336]), 0.0)
+    ts(X("te"), X("td"), X("ph"), A.mult)
+    fill(X("rst", s_[:, 0:160:16]), -BIG)
+    for c in range(8):
+        act(X("win", s_[:, 320 * c:320 * c + 320]), X("lm", s_[:, 512:832]), bias=X("te", s_[:, c:c + 1]))
     for a in range(4):
         select(X("lm", s_[32 * a:32 * a + 32, 0:512:4]), [[1, 4], [4, 32]], A.is_gt, 0.0, -a, -4)
-    for k in range(4):
-        act(X("win", s_[:, 640 * k:640 * k + 640]), X("hu", s_[:, 0:640]))
-    ts(X("pa"), X("pq"), 7, A.bitwise_and)
-    fill(X("rst"), 0.0)
-    copy(X("pm"), X("pa"))
-    fill(X("rst", s_[:, 0:160:16]), -BIG)
-    ts(X("uo"), X("ul"), X("pm", s_[:, 0:1]), A.add)
-    fill(X("fm", s_[:, 160:168]), 0.0)
-    fill(X("fm", s_[:, 320:328]), 0.0)
-    for b in range(4):
-        quant(Q("eq", EC * b, EC * b + EC), X("et", s_[:, 3 - b:3 - b + 4 * EC]))
     quant(Q("uq", 0, 128), X("ut"))
+    quant(Q("eq", 0, EC), X("et", s_[:, 3:3 + 4 * EC]))
     words = lambda x: (x[0].bitcast(dt.uint32), x[1])
     copy(words(X("u2")), by(words(X("uq")), X("uo")))
-    act(X("u2s"), by(X("us"), X("uo")))
+    copy(X("u2s"), by(X("us"), X("uo")))
     iota(X("val"), [[0, 4], [32, 5], [1, 16]], 0, 0)
     iota(X("va1"), [[0, 4], [32, 5], [1, 16]], 16, 0)
-    iota(X("va2"), [[1280, 2], [640, 2], [0, 80]], 0, 80)
-    iota(X("pj"), [[0, 2]], 0, 1, True)
+    iota(X("va2"), [[1280, 2], [640, 2], [0, 80]], 0, 0)
     iota(X("nn"), [[0, 32]], 0, 0)
-    dmas("dl", [("s", X("val", s_[16:128:32, :]), X("va1", s_[0:4, :])), ("s", X("val", s_[8:128:32, :]), X("va2", s_[0:128:32, :])),
-                ("s", X("val", s_[24:128:32, :]), X("va2", s_[0:128:32, :]))])
 
-    CC = X("cc", s_[:, 0:1])
+    def constants():
+        for b in range(1, 4):
+            quant(Q("eq", EC * b, EC * b + EC), X("et", s_[:, 3 - b:3 - b + 4 * EC]))
+            yield
+        quant(Q("hq", 0, 128), X("hu", s_[:, 0:512]))
+        yield
+
+    def more_constants():
+        ts(X("pb"), X("ti", s_[:, 0:1]), 4, A.arith_shift_right, 1, A.bitwise_and)
+        fill(X("c320"), 320.0)
+        yield
+        ts(X("cc"), X("pb"), -10240.0, A.mult, 40960.0, A.add)
+        quant(Q("lq", 0, 256), X("lm"))
+        yield
+        for name, n in (("mk8", 8), ("mg", 12), ("mk4", 4)):
+            fill(X(name), 1.0)
+            yield
+            fill(X(name, s_[:, 0::n]), 0.0)
+        for name, k, c in (("mg", 9, 1.0 / 320), ("mg", 11, -319.0), ("gb", 9, WHOLE), ("gb", 10, -WHOLE), ("gb", 11, 149.0)):
+            fill(X(name, s_[:, k::12]), c)
+        yield
+
+    def lay_lists():
+        dmas("dl", [("s", X("win0", s_[0:16, :]), X("win", s_[0:128:8, :])),
+                    ("s", X("val", s_[16:128:32, :]), X("va1", s_[0:4, :])), ("s", X("val", s_[8:128:16, :]), X("va2", s_[0:8, :]))])
+
+    CC = X("cc")
 
     def xh(h):
         return Q("xq", 160 * h, 160 * h + 160)
 
-    def quant_x(h):
+    def choose(h, beside=None):
+        n, m, lo = slice(10 * h, 10 * h + 10), slice(5 * h, 5 * h + 5), 160 * h
         quant(xh(h), X("xt", s_[:, 640 * h:640 * h + 640]))
-
-    def scores(h):
-        return mm(0, 160, Q("u2", 0, 128), xh(h))
-
-    def choose(h, p):
-        n, m = slice(10 * h, 10 * h + 10), slice(5 * h, 5 * h + 5)
-        lo = 160 * h
-        st, fm = X("st", s_[:, lo:lo + 160]), X("fm", s_[:, lo:lo + 160])
+        p = mm(2 * h, 160, Q("u2", 0, 128), xh(h))
+        if beside:
+            beside()
+        yield
+        st, fm = X("st", s_[:, lo:lo + 160]), X("fm", s_[:, 168 * h:168 * h + 160])
         turn32(st, p)
+        yield
         scan(fm, st, X("rst"), 0.0, A.max, A.add)
-        tt(X("gg", s_[:, n, :]), fm, X("fm", s_[:, lo + 7:lo + 167]), A.is_ge)
+        yield
+        tt(X("gg", s_[:, n, :]), fm, X("fm", s_[:, 168 * h + 7:168 * h + 167]), A.is_ge)
+        yield
         tt(X("gs", s_[:, m, :]), X("gg", s_[:, 10 * h:10 * h + 10:2, 0:9]), X("gg", s_[:, 10 * h + 1:10 * h + 10:2, 0:9]), A.add)
+        yield
         for k in range(4):
             o = 32 * (8 + 5 * h + k) + k
             tt(X("hu", s_[:, o:o + 160:4]), X("gs", s_[:, m, 1:9]), X("gs", s_[:, m, 0:8]), A.subtract)
+        yield
 
     def unpack(d, h):
         for b in range(4):
-            e, o = EC * b + 16 * d, 1280 * d + 640 * h + 160 * b
+            e, o = EC * b + 16 * d, 1280 * (d + 1) + 640 * h + 160 * b
             act(X("tw", s_[:, o:o + 160]), mm(bank(), 160, Q("eq", e, e + 128), xh(h)), 0.015625)
 
     def turn(ds, h, close=False):
         jobs = []
         for d in ds:
-            o = 1280 * d + 640 * h
-            jobs += [("s", X("tw", s_[64 * k:64 * k + 64, 5120 + o:5760 + o]), X("tw", s_[64 - 64 * k:128 - 64 * k, o:o + 640])) for k in range(2)]
+            o = 1280 * (d + 1) + 640 * h
+            for to in [o + 5120] + [640 * h] * (d == 3):
+                jobs += [("s", X("tw", s_[64 * k:64 * k + 64, to:to + 640]), X("tw", s_[64 - 64 * k:128 - 64 * k, o:o + 640])) for k in range(2)]
         dmas("rot", jobs, close)
 
-    quant_x(0)
-    p = scores(0)
-    quant(Q("hq", 0, 128), X("hu", s_[:, 0:512]))
-    choose(0, p)
-    unpack(0, 0)
-    quant_x(1)
-
-    for t in range(3):
-        p = scores(1)
-        if t == 0:
-            quant(Q("lq", 0, 256), X("lm"))
+    def window_early():
+        unpack(0, 0)
         unpack(1, 0)
         turn((0, 1), 0)
+
+    def window_mid():
+        unpack(3, 1)
         unpack(2, 1)
-        choose(1, p)
+        turn((3, 2), 1)
+
+    def window_late():
+        unpack(3, 0)
+        unpack(2, 0)
+        if 4 in OPT["pe"]:
+            turn((3, 2), 0, True)
+            for d in (0, 1, 4, 5):
+                unpack(d, 1)
+        else:
+            turn((3, 2), 0)
+            unpack(0, 1)
+            unpack(1, 1)
+            turn((0, 1), 1, True)
+
+    def places():
         quant(Q("hq", 64, 192), X("hu", s_[:, 256:768]))
         for k in range(3):
             mm(1, 128, Q("lq", 128 * min(k, 1), 128 * min(k, 1) + 128), Q("hq", 64 - 32 * k, 192 - 32 * k), k == 0, k == 2)
-        unpack(3, 1)
-        turn((2, 3), 1)
-        unpack(2, 0)
-        unpack(3, 0)
-        turn((2, 3), 0, True)
-        for d in (0, 1, 4, 5):
-            unpack(d, 1)
-        if t == 0:
-            for name, n in (("mk8", 8), ("mk9", 9), ("mk4", 4)):
-                fill(X(name), 1.0)
-                fill(X(name, s_[:, 0::n]), 0.0)
-            fill(X("c320"), 320.0)
+        window_late()
         A0 = X("p1", s_[:, 0:80])
+        tt(X("h0"), X("gg", s_[:, 0:20:2, 1:9]), X("gg", s_[:, 0:20:2, 0:8]), A.subtract)
         for e in range(2):
             ts(X("dd", s_[:, 80 * e:80 * e + 80]), X("gg", s_[:, e:20:2, 0:8]), -STEP - FAR, A.mult, FAR, A.add)
-        tt(X("h0"), X("gg", s_[:, 0:20:2, 1:9]), X("gg", s_[:, 0:20:2, 0:8]), A.subtract)
         scan(X("th"), X("dd"), X("c320"), 0.0, A.add, A.min)
         tt(X("a1"), A0, X("h0"), A.add)
-        ts(X("rl"), A0, 320.0, A.max, 8.5 / 8 - 320.0, A.add)
-        scan(X("pk", s_[:, 0:80]), X("dd", s_[:, 0:80]), A0, 0.0, A.add, A.min)
         ts(X("occ"), X("p1", s_[:, 80:88]), 320.0, A.min)
+        ts(X("rl", s_[:, 0:80]), A0, 320.0, A.max, 8.5 / 8 - 320.0, A.add)
+        scan(X("pk", s_[:, 0:80]), X("dd", s_[:, 0:80]), A0, 0.0, A.add, A.min)
+        ts(X("rl", s_[:, 80:160]), X("a1"), 320.0, A.max, 8.5 / 8 - 320.0, A.add)
         scan(X("pk", s_[:, 80:160]), X("dd", s_[:, 80:160]), X("a1"), 0.0, A.add, A.min)
-        scan(X("rs", s_[:, 0:80]), X("mk8"), X("rl"), 0.0, A.mult, A.add)
         scan(X("fb"), X("c320", s_[:, 0:8]), X("occ"), 8.5, A.add, A.subtract)
-        F, TH, O0 = X("pk", s_[:, 7:160:8]), X("th", s_[:, 7:160:8]), X("occ", s_[:, 0:1])
-        tt(X("rj"), F, TH, A.is_ge)
+        ts(X("wv"), X("occ"), STEP - 320.0, A.add, 20.0, A.mult)
+        scan(X("rs"), X("mk8"), X("rl"), 0.0, A.mult, A.add)
+        F, TH, R = X("pk", s_[:, 7:160:8]), X("th", s_[:, 7:160:8]), X("rs", s_[:, 7:160:8])
         tt(X("ac"), F, TH, A.is_lt)
-        ts(X("fp"), F, 7 * STEP + 8.5, A.add, O0, A.subtract)
-        ts(X("wv"), X("occ"), STEP - 320.0, A.add)
-        tt(X("rs", s_[:, 87:160:8]), X("rs", s_[:, 7:80:8]), X("rj", s_[:, 0:10]), A.add)
-        tt(X("gb", s_[:, 1:180:9]), X("fp"), X("ac"), A.mult)
-        FF = X("gb", s_[:, 0:180:9])
-        tt(FF, X("rs", s_[:, 7:160:8]), X("rj"), A.mult)
+        ts(X("fp"), F, 7 * STEP + 8.5, A.add, 20.0, A.mult)
+        tt(X("mg", s_[:, 8:240:12]), F, TH, A.is_ge)
+        ts(X("gb", s_[:, 0:240:12]), R, X("occ", s_[:, 0:1]), A.add, 20.0, A.mult)
         for c in range(1, 8):
-            ts(X("gb", s_[:, c + 1:180:9]), FF, X("fb", s_[:, c - 1:c]), A.is_ge, X("wv", s_[:, c:c + 1]), A.mult)
-        scan(X("gt"), X("mk9"), X("gb"), 0.0, A.mult, A.add)
-        GT = X("gt", s_[:, 8:180:9])
-        ts(X("m1"), GT, O0, A.add, 0.0625, A.mult)
-        ts(X("z1"), GT, O0, A.add, 20.0, A.mult)
-        ts(X("z2"), X("m1"), -319.0, A.mult, 149.0, A.add)
-        tt(X("z3"), X("z1"), X("z2"), A.add)
+            if c == 4:
+                tt(X("gb", s_[:, 8:240:12]), X("fp"), X("ac"), A.mult)
+            ts(X("gb", s_[:, c:240:12]), R, X("fb", s_[:, c - 1:c]), A.is_ge, X("wv", s_[:, c:c + 1]), A.mult)
+        scan(X("gt"), X("mg"), X("gb"), 0.0, A.mult, A.add)
+        tt(X("z3"), X("gt", s_[:, 8:240:12]), X("gt", s_[:, 11:240:12]), A.add)
         copy(X("sl"), X("z3"))
         op("v", lambda: V.tensor_copy(T.win[:].indirect(T.sl[:]), T.val[:]), [X("sl"), X("val")], [X("win")])
-        for k in range(20):
-            turn32(X("wt", s_[:, 128 * k:128 * k + 128]), X("win", s_[:, k:2560:20]))
-        if t == 0:
-            ts(X("pb"), X("pj"), 4, A.arith_shift_right)
-        scan(X("s4"), X("mk4"), X("wt", s_[:, 0:2560:8]), 0.0, A.mult, A.add)
-        if t == 0:
-            ts(X("cc"), X("pb"), 1280.0, A.mult)
-        tt(X("u1", s_[0:64]), X("s4", s_[0:64, 3:320:4]), X("s4", s_[64:128, 3:320:4]), A.add)
-        for a in range(4):
-            tt(X("w3", s_[32 * a:32 * a + 32]), X("u1", s_[0:32, a:80:4]), X("u1", s_[32:64, a:80:4]), A.add)
-        ts(X("ng"), X("w3"), CC, A.is_lt, 10240.0, A.mult)
-        tt(X("sv"), X("w3"), X("ng"), A.add)
-        ts(X("gl"), X("sv"), CC, A.subtract)
 
-        def gather(h):
-            for b in (0, 2, 1, 3):
-                o = X("yt", s_[:, 640 * h + b:640 * h + 640:4])
-                i = by(X("tw", s_[:, 160 * b:160 * b + 9760]), X("gl", s_[:, 10 * h:10 * h + 10]))
-                if b < 2:
-                    copy(o, i)
-                else:
-                    act(o, i)
-        gather(1)
+    def turns(ks):
+        for k in ks:
+            turn32(X("wt", s_[:, 128 * k:128 * k + 128]), X("win", s_[:, k:2560:20]))
+
+    def sources(h):
+        scan(X("s4", s_[:, 160 * h:160 * h + 160]), X("mk4"), X("wt", s_[:, 1280 * h:1280 * h + 1280:8]), 0.0, A.mult, A.add)
+        yield
+        tt(X("u1", s_[0:64, 40 * h:40 * h + 40]), X("s4", s_[0:64, 160 * h + 3:160 * h + 160:4]), X("s4", s_[64:128, 160 * h + 3:160 * h + 160:4]), A.add)
+        yield
+        for a in range(4):
+            k = slice(40 * h + a, 40 * h + 40, 4)
+            tt(X("w3", s_[32 * a:32 * a + 32, 10 * h:10 * h + 10]), X("u1", s_[0:32, k]), X("u1", s_[32:64, k]), A.add)
+        yield
+        ts(X("gl", s_[:, 10 * h:10 * h + 10]), X("w3", s_[:, 10 * h:10 * h + 10]), CC, A.add)
+        yield
+        for b in (0, 2, 1, 3):
+            o = X("yt", s_[:, 640 * h + b:640 * h + 640:4])
+            i = by(X("tw", s_[:, 160 * b:160 * b + 11040]), X("gl", s_[:, 10 * h:10 * h + 10]))
+            if b < 2:
+                copy(o, i)
+            else:
+                act(o, i)
+        yield
+
+    def cross(t):
+        yield from sources(1)
         out, land = Q("ac%d" % t, 0, 160), Q("lc%d" % t, 0, 160)
         quant(out, X("yt", s_[:, 640:1280]))
         dst = T.cores[rank ^ ROUNDS[t]]
@@ -355,10 +401,17 @@ def rank_program(g, core, T, topo):
         snap[("arr%d" % t, 16)] = {}
         note(("arr%d" % t, 16), [], feet(land))
         cnt["arr%d" % t] = cnt["snt%d" % t] = 16
-        if t < 2:
-            iota(X("win"), [[0, 2560]], 0, 0)
+        yield
 
-        gather(0)
+    def stay_list(t):
+        for ks in ((0, 1, 2, 3), (4, 5, 6, 7), (8, 9)):
+            turns(ks)
+            yield
+        if t < 2:
+            dmas("dz", [("s", X("win", s_[0:128:8, :]), X("win0", s_[0:16, :]))])
+        yield from sources(0)
+
+    def layer_stay():
         quant(Q("zq", 0, 160), X("yt", s_[:, 0:640]))
         for b in (2, 3, 0, 1):
             act(X("y64", s_[:, b:640:4]), X("yt", s_[:, b:640:4]), 64.0)
@@ -366,22 +419,9 @@ def rank_program(g, core, T, topo):
             p = mm(bank(), 160, Q("wq", 128 * b, 128 * b + 128), Q("zq", 0, 160))
             tt(X("t64", s_[:, 160 * b:160 * b + 160]), p, X("y64", s_[:, b:640:4]), A.add)
             act(X("xt", s_[:, b:640:4]), X("t64", s_[:, 160 * b:160 * b + 160]), 0.015625)
-        if t == 1:
-            quant(Q("vq", 0, 128), X("vt"))
-        quant_x(0)
-        if t < 2:
-            choose(0, scores(0))
-        else:
-            p = mm(0, 160, Q("vq", 0, 128), xh(0))
-            ts(X("gi"), X("w3"), -400.0, A.add, 0.00078125, A.mult)
-            ts(X("mi"), X("w3"), -80.0, A.add, 0.0015625, A.mult)
-            ts(X("n8"), X("w3"), 8.0, A.mult)
-            act(X("yo", s_[:, 0:160]), p)
-            ts(X("n1"), X("gi"), -2559.0, A.mult)
-            ts(X("n2"), X("mi"), -3840.0, A.mult)
-            tt(X("n3"), X("n8"), X("n1"), A.add)
-            tt(X("nn", s_[:, 0:20]), X("n3"), X("n2"), A.add)
-            turn32(X("omt"), X("nn"))
+
+    def layer_arrived(t):
+        land = Q("lc%d" % t, 0, 160)
         for b in range(4):
             k = bank()
             mm(k, 160, Q("wq", 128 * b, 128 * b + 128), land, True, False)
@@ -391,9 +431,52 @@ def rank_program(g, core, T, topo):
                 ts(o, p, 0.015625, A.mult)
             else:
                 act(o, p, 0.015625)
-        if t < 2:
-            unpack(0, 0)
-        quant_x(1)
+
+    def later(n, chain):
+        for k in range(n):
+            yield
+        yield from chain
+
+    weave(choose(0), constants())
+    window_early()
+    weave(choose(1, window_mid), more_constants())
+    lay_lists()
+    for t in range(3):
+        places()
+        turns(range(10, 20))
+        weave(cross(t), stay_list(t))
+        layer_stay()
+        if t == 0:
+            quant(Q("vq", 0, 128), X("vt"))
+        if t < 2 and t in OPT["rfirst"]:
+            layer_arrived(t)
+            weave(choose(0), later(OPT.get("lag", 1), choose(1, lambda: (window_early(), window_mid()))))
+        elif t < 2:
+            weave(choose(0))
+            layer_arrived(t)
+            window_early()
+            weave(choose(1, window_mid))
+
+    ts(X("n1"), X("w3"), CC, A.add)
+    ts(X("pd"), X("ti", s_[:, 0:1]), 4, A.arith_shift_right)
+    quant(xh(0), X("xt", s_[:, 0:640]))
+    p = mm(0, 160, Q("vq", 0, 128), xh(0))
+    act(X("yo", s_[:, 0:160]), p)
+    ts(X("gi"), X("n1"), -400.0, A.add, 0.00078125, A.mult)
+    ts(X("mi"), X("n1"), -80.0, A.add, 0.0015625, A.mult)
+    ts(X("ph"), X("pd"), 7.0, A.add)
+    ts(X("n2"), X("n1"), 8.0, A.mult)
+    ts(X("n3"), X("mi"), -3840.0, A.mult)
+    ts(X("n4"), X("gi"), -2560.0, A.mult)
+    ts(X("gj"), X("gi"), X("ph"), A.add)
+    tt(X("n5"), X("n2"), X("n3"), A.add)
+    ts(X("gk"), X("gj"), 7, A.bitwise_and)
+    tt(X("n6"), X("n5"), X("n4"), A.add)
+    tt(X("nn", s_[:, 0:20]), X("n6"), X("gk"), A.add)
+    turn32(X("omt"), X("nn"))
+    layer_arrived(2)
+    quant(xh(1), X("xt", s_[:, 640:1280]))
+    p = mm(1, 160, Q("vq", 0, 128), xh(1))
 
     def store_q(h, q1, q2):
         lo, hi = 160 * h, 160 * h + 160
@@ -403,7 +486,7 @@ def rank_program(g, core, T, topo):
     jobs = store_q(0, "s", "s")
     jobs += [("s", hbm(T.y[:, 0:160]), X("yo", s_[:, 0:160]))]
     jobs += [("s", hbm(T.om[c:c + 1, :]), X("omt", s_[32 * (c // 2):32 * (c // 2) + 20, 16 * (c % 2):16 * (c % 2) + 16])) for c in range(8)]
-    copy(X("yo", s_[:, 160:320]), mm(1, 160, Q("vq", 0, 128), xh(1)))
+    copy(X("yo", s_[:, 160:320]), p)
     jobs += store_q(1, "s", "a")
     jobs += [("s", hbm(T.y[:, 160:320]), X("yo", s_[:, 160:320]))]
     dmas("outs", jobs)

@@ -8,7 +8,7 @@ STEP = 5120.0
 WHOLE = 12582912.0
 EC = 208
 SCRATCH = {}
-OPT = {"rfirst": (1,),  "pe": (0, 1, 4, 5)}
+OPT = {"rfirst": (0, 1), "pe": (0, 1, 4, 5)}
 
 
 def _declare(where, dtype, text):
@@ -17,10 +17,10 @@ def _declare(where, dtype, text):
         SCRATCH[name] = (where, [128] + [int(k) for k in dims.split("x")], dtype)
 
 
-_declare("sbuf", "bfloat16", "xt:1280 yt:1280 y64:640 ut:512 vt:512 et:%d lm:1024 hu:768 tw:11520 gg:20x16 gs:10x9 h0:80 dd:160 "
+_declare("sbuf", "bfloat16", "xt:1280 yt:1280 y64:640 ut:512 vt:512 et:%d lm:1024 hu:768 tw:11520 tw2:1280 gg:20x16 gs:10x9 h0:80 dd:160 "
          "c320:160 mk8:160 mk4:160 val:320 va1:320 va2:320 win:2560 win0:2560 wt:2560" % (4 * EC + 8))
 _declare("sbuf", "float32", "st:320 fm:336 rst:160 pk:160 th:160 wv:8 z3:20 a1:80 rl:160 rs:160 occ:8 fb:8 ac:20 fp:20 gb:240 gt:240 mg:240 "
-         "s4:320 u1:80 w3:20 cc:1 pm:1 ph:1 ul:8 tb:8 tc:8 td:8 te:8 n1:20 n2:20 n3:20 n4:20 n5:20 n6:20 nn:32 omt:32 yo:320 t64:640")
+         "s4:320 u1:80 w3:20 cc:1 c4:1 c8:1 pm:1 ph:1 pt:1 tr:128 ul:8 tb:8 tc:8 td:8 te:8 n1:20 n2:20 n3:20 n4:20 n5:20 n6:20 nn:32 omt:32 yo:320 t64:640")
 _declare("sbuf", "int32", "pa:1 pb:1 pc:1 pd:1 ti:16 tj:8 gi:20 mi:20 gj:20 gk:20")
 _declare("sbuf", "uint16", "sl:20 gl:20 uo:8")
 PAIRS = [("xq", "xs", 320), ("uq", "us", 128), ("u2", "u2s", 128), ("vq", "vs", 128), ("wq", "wsc", 512), ("eq", "es", 4 * EC), ("lq", "lqs", 256),
@@ -199,67 +199,68 @@ def rank_program(g, core, T, topo):
     def select(o, pattern, k, c, base, step):
         op("p", lambda: g.affine_select(o[0], o[0], pattern, k, c, base, step), [o], [o])
 
-    dmas("dx0", [("s", X("xt", s_[:, 0:640]), hbm(T.x[:, 0:640]))])
-    dmas("du", [("a", X("ut"), hbm(T.u[:]))])
+    dmas("du", [("s", X("ut"), hbm(T.u[:]))])
+    dmas("dx0", [("a", X("xt", s_[:, 0:640]), hbm(T.x[:, 0:640]))])
     dmas("dx1", [("s", X("xt", s_[:, 640:1280]), hbm(T.x[:, 640:1280]))])
     dmas("dw", [("s", raw(X("wq")), hbm(T.wc[:])), ("s", X("wsc"), hbm(T.ws[:]))])
     dmas("dv", [("s", X("vt"), hbm(T.v[:]))])
 
     fill(X("et"), 0.0)
     iota(X("ti"), [[-32, 4], [0, 2], [7, 2]], 128, 1, True)
-    iota(X("tb"), [[0, 4], [1280, 2]], -1280, 0)
     iota(X("ul"), [[16, 8]], 0, 0)
+    for k in range(2):
+        fill(X("tb", s_[:, k::2]), 7680.0 + 1280.0 * k)
     for lo, hi in ((0, 128), (128, EC)):
         select(X("et", s_[:, 4 * lo + 3:4 * hi:4]), [[-1, hi - lo]], A.not_equal, 64.0, 0, 1)
-    fill(X("lm"), 1.0)
+    iota(X("tr"), [[1, 4], [4, 32]], 0, -4)
+    ts(X("pa"), X("ti", s_[:, 1:2]), 7, A.bitwise_and)
     ts(X("tj"), X("ti", s_[:, 0:16:2]), 5, A.arith_shift_right, 3, A.bitwise_and)
     ts(X("pc"), X("ti", s_[:, 0:1]), 3, A.arith_shift_right, 1, A.bitwise_and)
-    ts(X("pa"), X("ti", s_[:, 1:2]), 7, A.bitwise_and)
-    fill(X("hu"), 0.0)
+    fill(X("rst"), 0.0)
+    copy(X("pm"), X("pa"))
     ts(X("tc"), X("tj"), -2560.0, A.mult)
     copy(X("ph"), X("pc"))
-    copy(X("pm"), X("pa"))
-    fill(X("rst"), 0.0)
-    tt(X("td"), X("tc"), X("tb"), A.add)
-    ts(X("uo"), X("ul"), X("pm"), A.add)
-    fill(X("fm", s_[:, 160:168]), 0.0)
-    fill(X("fm", s_[:, 328:336]), 0.0)
-    ts(X("te"), X("td"), X("ph"), A.mult)
     fill(X("rst", s_[:, 0:160:16]), -BIG)
+    ts(X("uo"), X("ul"), X("pm"), A.add)
+    tt(X("td"), X("tc"), X("tb"), A.add)
+    fill(X("hu"), 0.0)
+    ts(X("te"), X("td"), X("ph"), A.mult)
+    for k in range(2):
+        op("a", lambda: S.activation(T.lm[:, 512 * k:512 * k + 512], T.hu[:, 0:512], AF.Identity, bias=1.0), [X("hu", s_[:, 0:512])], [X("lm", s_[:, 512 * k:512 * k + 512])])
     for c in range(8):
         act(X("win", s_[:, 320 * c:320 * c + 320]), X("lm", s_[:, 512:832]), bias=X("te", s_[:, c:c + 1]))
-    for a in range(4):
-        select(X("lm", s_[32 * a:32 * a + 32, 0:512:4]), [[1, 4], [4, 32]], A.is_gt, 0.0, -a, -4)
+    for k in (160, 328):
+        fill(X("fm", s_[:, k:k + 8]), 0.0)
+    fill(X("c320"), 320.0)
+    for k, c in ((9, WHOLE), (10, -WHOLE), (11, 149.0)):
+        fill(X("gb", s_[:, k::12]), c)
     quant(Q("uq", 0, 128), X("ut"))
-    quant(Q("eq", 0, EC), X("et", s_[:, 3:3 + 4 * EC]))
+    ts(X("pd"), X("ti", s_[:, 0:1]), 5, A.arith_shift_right)
+    ts(X("pb"), X("ti", s_[:, 0:1]), 4, A.arith_shift_right, 1, A.bitwise_and)
     words = lambda x: (x[0].bitcast(dt.uint32), x[1])
     copy(words(X("u2")), by(words(X("uq")), X("uo")))
     copy(X("u2s"), by(X("us"), X("uo")))
     iota(X("val"), [[0, 4], [32, 5], [1, 16]], 0, 0)
     iota(X("va1"), [[0, 4], [32, 5], [1, 16]], 16, 0)
     iota(X("va2"), [[1280, 2], [640, 2], [0, 80]], 0, 0)
+    iota(X("mk8"), [[0, 20], [30000, 8]], 0, 0)
+    iota(X("mg"), [[0, 240]], 1, 0)
+    for k, c in ((0, 0), (11, -319)):
+        iota(X("mg", s_[:, k::12]), [[0, 20]], c, 0)
+    iota(X("mk4"), [[0, 40], [30000, 4]], 0, 0)
     iota(X("nn"), [[0, 32]], 0, 0)
 
     def constants():
-        for b in range(1, 4):
+        ts(X("pt"), X("pd"), -127.0, A.mult, 508.0, A.add)
+        for b in range(4):
             quant(Q("eq", EC * b, EC * b + EC), X("et", s_[:, 3 - b:3 - b + 4 * EC]))
-            yield
-        quant(Q("hq", 0, 128), X("hu", s_[:, 0:512]))
+            if b == 2:
+                ts(X("lm", s_[:, 0:512:4]), X("tr"), X("pt"), A.is_gt)
+            if b:
+                yield
         yield
-
-    def more_constants():
-        ts(X("pb"), X("ti", s_[:, 0:1]), 4, A.arith_shift_right, 1, A.bitwise_and)
-        fill(X("c320"), 320.0)
-        yield
-        ts(X("cc"), X("pb"), -10240.0, A.mult, 40960.0, A.add)
         quant(Q("lq", 0, 256), X("lm"))
-        yield
-        for name, n in (("mk8", 8), ("mg", 12), ("mk4", 4)):
-            fill(X(name), 1.0)
-            yield
-            fill(X(name, s_[:, 0::n]), 0.0)
-        for name, k, c in (("mg", 9, 1.0 / 320), ("mg", 11, -319.0), ("gb", 9, WHOLE), ("gb", 10, -WHOLE), ("gb", 11, 149.0)):
-            fill(X(name, s_[:, k::12]), c)
+        ts(X("cc"), X("pb"), -10240.0, A.mult, 40960.0 - 7 * 8960.0, A.add)
         yield
 
     def lay_lists():
@@ -303,6 +304,8 @@ def rank_program(g, core, T, topo):
             o = 1280 * (d + 1) + 640 * h
             for to in [o + 5120] + [640 * h] * (d == 3):
                 jobs += [("s", X("tw", s_[64 * k:64 * k + 64, to:to + 640]), X("tw", s_[64 - 64 * k:128 - 64 * k, o:o + 640])) for k in range(2)]
+            if OPT.get("dup") and d < 2:
+                jobs += [("s", X("tw2", s_[64 * k:64 * k + 64, 640 * d:640 * d + 640]), X("tw", s_[64 - 64 * k:128 - 64 * k, o:o + 640])) for k in range(2)]
         dmas("rot", jobs, close)
 
     def window_early():
@@ -320,7 +323,7 @@ def rank_program(g, core, T, topo):
         unpack(2, 0)
         if 4 in OPT["pe"]:
             turn((3, 2), 0, True)
-            for d in (0, 1, 4, 5):
+            for d in (0, 1, 4, 5) + OPT.get("more", ()):
                 unpack(d, 1)
         else:
             turn((3, 2), 0)
@@ -328,10 +331,14 @@ def rank_program(g, core, T, topo):
             unpack(1, 1)
             turn((0, 1), 1, True)
 
-    def places():
-        quant(Q("hq", 64, 192), X("hu", s_[:, 256:768]))
+    def places(t):
+        lo = 64 if t else 0
+        quant(Q("hq", lo, 192), X("hu", s_[:, 4 * lo:768]))
         for k in range(3):
             mm(1, 128, Q("lq", 128 * min(k, 1), 128 * min(k, 1) + 128), Q("hq", 64 - 32 * k, 192 - 32 * k), k == 0, k == 2)
+        if t == 0:
+            window_mid()
+            fill(X("mg", s_[:, 9::12]), 1.0 / 320)
         window_late()
         A0 = X("p1", s_[:, 0:80])
         tt(X("h0"), X("gg", s_[:, 0:20:2, 1:9]), X("gg", s_[:, 0:20:2, 0:8]), A.subtract)
@@ -346,7 +353,7 @@ def rank_program(g, core, T, topo):
         scan(X("pk", s_[:, 80:160]), X("dd", s_[:, 80:160]), X("a1"), 0.0, A.add, A.min)
         scan(X("fb"), X("c320", s_[:, 0:8]), X("occ"), 8.5, A.add, A.subtract)
         ts(X("wv"), X("occ"), STEP - 320.0, A.add, 20.0, A.mult)
-        scan(X("rs"), X("mk8"), X("rl"), 0.0, A.mult, A.add)
+        scan(X("rs"), X("mk8"), X("rl"), 0.0, A.min, A.add)
         F, TH, R = X("pk", s_[:, 7:160:8]), X("th", s_[:, 7:160:8]), X("rs", s_[:, 7:160:8])
         tt(X("ac"), F, TH, A.is_lt)
         ts(X("fp"), F, 7 * STEP + 8.5, A.add, 20.0, A.mult)
@@ -366,7 +373,7 @@ def rank_program(g, core, T, topo):
             turn32(X("wt", s_[:, 128 * k:128 * k + 128]), X("win", s_[:, k:2560:20]))
 
     def sources(h):
-        scan(X("s4", s_[:, 160 * h:160 * h + 160]), X("mk4"), X("wt", s_[:, 1280 * h:1280 * h + 1280:8]), 0.0, A.mult, A.add)
+        scan(X("s4", s_[:, 160 * h:160 * h + 160]), X("mk4"), X("wt", s_[:, 1280 * h:1280 * h + 1280:8]), 0.0, A.min, A.add)
         yield
         tt(X("u1", s_[0:64, 40 * h:40 * h + 40]), X("s4", s_[0:64, 160 * h + 3:160 * h + 160:4]), X("s4", s_[64:128, 160 * h + 3:160 * h + 160:4]), A.add)
         yield
@@ -412,13 +419,34 @@ def rank_program(g, core, T, topo):
         yield from sources(0)
 
     def layer_stay():
+        yield
         quant(Q("zq", 0, 160), X("yt", s_[:, 0:640]))
         for b in (2, 3, 0, 1):
             act(X("y64", s_[:, b:640:4]), X("yt", s_[:, b:640:4]), 64.0)
+        yield
         for b in (2, 3, 0, 1):
             p = mm(bank(), 160, Q("wq", 128 * b, 128 * b + 128), Q("zq", 0, 160))
             tt(X("t64", s_[:, 160 * b:160 * b + 160]), p, X("y64", s_[:, b:640:4]), A.add)
             act(X("xt", s_[:, b:640:4]), X("t64", s_[:, 160 * b:160 * b + 160]), 0.015625)
+        yield
+
+    def numbers():
+        ts(X("gi"), X("w3"), X("c4"), A.add, 0.00078125, A.mult)
+        ts(X("mi"), X("w3"), X("c8"), A.add, 0.0015625, A.mult)
+        ts(X("n2"), X("w3"), CC, A.add, 8.0, A.mult)
+        yield
+        ts(X("gj"), X("gi"), X("ph"), A.add)
+        ts(X("n3"), X("mi"), -3840.0, A.mult)
+        ts(X("n4"), X("gi"), -2560.0, A.mult)
+        ts(X("gk"), X("gj"), 7, A.bitwise_and)
+        tt(X("n5"), X("n2"), X("n3"), A.add)
+        tt(X("n6"), X("gk"), X("n4"), A.add)
+        yield
+        tt(X("nn", s_[:, 0:20]), X("n6"), X("n5"), A.add)
+        yield
+        turn32(X("omt"), X("nn"))
+        dmas("outs", [("s", hbm(T.om[c:c + 1, :]), X("omt", s_[32 * (c // 2):32 * (c // 2) + 20, 16 * (c % 2):16 * (c % 2) + 16])) for c in range(8)], False)
+        yield
 
     def layer_arrived(t):
         land = Q("lc%d" % t, 0, 160)
@@ -437,58 +465,36 @@ def rank_program(g, core, T, topo):
             yield
         yield from chain
 
-    weave(choose(0), constants())
-    window_early()
-    weave(choose(1, window_mid), more_constants())
+    weave(choose(0), choose(1), constants())
     lay_lists()
+    window_early()
     for t in range(3):
-        places()
+        places(t)
         turns(range(10, 20))
         weave(cross(t), stay_list(t))
-        layer_stay()
+        weave(layer_stay(), numbers() if t == 2 else iter(()))
         if t == 0:
             quant(Q("vq", 0, 128), X("vt"))
+            ts(X("pd"), X("ti", s_[:, 0:1]), 4, A.arith_shift_right)
+            ts(X("c4"), CC, -400.0, A.add)
+            ts(X("c8"), CC, -80.0, A.add)
+            ts(X("ph"), X("pd"), 7.0, A.add)
         if t < 2 and t in OPT["rfirst"]:
             layer_arrived(t)
             weave(choose(0), later(OPT.get("lag", 1), choose(1, lambda: (window_early(), window_mid()))))
         elif t < 2:
-            weave(choose(0))
+            weave(choose(0, window_early))
             layer_arrived(t)
-            window_early()
             weave(choose(1, window_mid))
 
-    ts(X("n1"), X("w3"), CC, A.add)
-    ts(X("pd"), X("ti", s_[:, 0:1]), 4, A.arith_shift_right)
     quant(xh(0), X("xt", s_[:, 0:640]))
-    p = mm(0, 160, Q("vq", 0, 128), xh(0))
-    act(X("yo", s_[:, 0:160]), p)
-    ts(X("gi"), X("n1"), -400.0, A.add, 0.00078125, A.mult)
-    ts(X("mi"), X("n1"), -80.0, A.add, 0.0015625, A.mult)
-    ts(X("ph"), X("pd"), 7.0, A.add)
-    ts(X("n2"), X("n1"), 8.0, A.mult)
-    ts(X("n3"), X("mi"), -3840.0, A.mult)
-    ts(X("n4"), X("gi"), -2560.0, A.mult)
-    ts(X("gj"), X("gi"), X("ph"), A.add)
-    tt(X("n5"), X("n2"), X("n3"), A.add)
-    ts(X("gk"), X("gj"), 7, A.bitwise_and)
-    tt(X("n6"), X("n5"), X("n4"), A.add)
-    tt(X("nn", s_[:, 0:20]), X("n6"), X("gk"), A.add)
-    turn32(X("omt"), X("nn"))
     layer_arrived(2)
+    act(X("yo", s_[:, 0:160]), mm(0, 160, Q("vq", 0, 128), xh(0)))
     quant(xh(1), X("xt", s_[:, 640:1280]))
-    p = mm(1, 160, Q("vq", 0, 128), xh(1))
-
-    def store_q(h, q1, q2):
-        lo, hi = 160 * h, 160 * h + 160
-        return [(q1, hbm(T.oc[:, 4 * lo:4 * hi]), raw(X("xq", s_[:, lo:hi])))] + \
-               [(q2, hbm(T.osc[4 * k:4 * k + 4, lo:hi]), X("xs", s_[32 * k:32 * k + 4, lo:hi])) for k in range(4)]
-
-    jobs = store_q(0, "s", "s")
-    jobs += [("s", hbm(T.y[:, 0:160]), X("yo", s_[:, 0:160]))]
-    jobs += [("s", hbm(T.om[c:c + 1, :]), X("omt", s_[32 * (c // 2):32 * (c // 2) + 20, 16 * (c % 2):16 * (c % 2) + 16])) for c in range(8)]
-    copy(X("yo", s_[:, 160:320]), p)
-    jobs += store_q(1, "s", "a")
-    jobs += [("s", hbm(T.y[:, 160:320]), X("yo", s_[:, 160:320]))]
+    copy(X("yo", s_[:, 160:320]), mm(1, 160, Q("vq", 0, 128), xh(1)))
+    jobs = [("s", hbm(T.oc[:, 640 * h:640 * h + 640]), raw(xh(h)[0])) for h in range(2)]
+    jobs += [("as"[h], hbm(T.y[:, 160 * h:160 * h + 160]), X("yo", s_[:, 160 * h:160 * h + 160])) for h in range(2)]
+    jobs += [("a", hbm(T.osc[4 * k:4 * k + 4, :]), X("xs", s_[32 * k:32 * k + 4, :])) for k in range(4)]
     dmas("outs", jobs)
     for s in SEMAPHORES:
         if cnt.get(s, 0) > clock["p"].get(s, 0):

@@ -1,4 +1,5 @@
 import numpy as np
+from concourse.bass import DstId, RemoteDMATransfer
 from concourse.mybir import dt, AluOpType as A, ActivationFunctionType as AF
 
 ROUNDS = [1, 2, 4]
@@ -6,9 +7,10 @@ BIG = float(2.0 ** 75)
 FAR = 65536.0
 STEP = 5120.0
 WHOLE = 12582912.0
-EC = 208
+TERMS = 13
+EC = 192
 SCRATCH = {}
-OPT = {"rfirst": (0, 1), "pe": (0, 1, 4, 5)}
+OPT = {"lag": (1, 0), "we": 2, "ev": ((), (0, 1), (0, 2)), "ord": ("kkrkkrkrkr", "krkkrkrkrkrk"), "or0": "krckrkrkrkcrk", "hs": 2, "wl": 1, "e0": 2, "tk": ((0, 1, 2), (3, 4, 5), (6, 7, 8, 9), ()), "pe": (1, 0, 4), "last": 1}
 
 
 def _declare(where, dtype, text):
@@ -18,9 +20,9 @@ def _declare(where, dtype, text):
 
 
 _declare("sbuf", "bfloat16", "xt:1280 yt:1280 y64:640 ut:512 vt:512 et:%d lm:1024 hu:768 tw:11520 tw2:1280 gg:20x16 gs:10x9 h0:80 dd:160 "
-         "c320:160 mk8:160 mk4:160 val:320 va1:320 va2:320 win:2560 win0:2560 wt:2560" % (4 * EC + 8))
-_declare("sbuf", "float32", "st:320 fm:336 rst:160 pk:160 th:160 wv:8 z3:20 a1:80 rl:160 rs:160 occ:8 fb:8 ac:20 fp:20 gb:240 gt:240 mg:240 "
-         "s4:320 u1:80 w3:20 cc:1 c4:1 c8:1 pm:1 ph:1 pt:1 tr:128 ul:8 tb:8 tc:8 td:8 te:8 n1:20 n2:20 n3:20 n4:20 n5:20 n6:20 nn:32 omt:32 yo:320 t64:640")
+         "c320:160 mk4:160 val:320 va1:320 va2:320 win:2560 win0:320 wt:2560" % (4 * EC + 8))
+_declare("sbuf", "float32", "st:320 fm:336 rst:160 pk:160 th:160 mk8:160 wv:8 z3:20 h1:80 same:10 of:20 nf:20 rl:160 rs:160 occ:8 fb:8 gb:260 gt:260 mg:260 "
+         "s4:320 u1:80 w3:20 cc:1 c4:1 c8:1 pm:1 ph:1 pt:1 tq:1 tr:128 ul:8 tb:8 tc:8 td:8 te:8 n1:20 n2:20 n3:20 n4:20 n5:20 n6:20 nn:32 omt:32 yo:320 t64:640")
 _declare("sbuf", "int32", "pa:1 pb:1 pc:1 pd:1 ti:16 tj:8 gi:20 mi:20 gj:20 gk:20")
 _declare("sbuf", "uint16", "sl:20 gl:20 uo:8")
 PAIRS = [("xq", "xs", 320), ("uq", "us", 128), ("u2", "u2s", 128), ("vq", "vs", 128), ("wq", "wsc", 512), ("eq", "es", 4 * EC), ("lq", "lqs", 256),
@@ -31,7 +33,7 @@ for _n, _s, _w in PAIRS:
 PLANE = {_n: _s for _n, _s, _w in PAIRS}
 for _t in range(8):
     SCRATCH["p%d" % _t] = ("psum", [128, 512], "float32")
-SEMAPHORES = ["qv", "qt", "qa", "qp", "dx0", "dx1", "du", "dv", "dw", "dl", "dz", "rot", "outs", "arr0", "arr1", "arr2", "snt0", "snt1", "snt2"]
+SEMAPHORES = ["qv", "qt", "qa", "qp", "dx0", "dx1", "du", "dv", "dw", "dl", "dq", "dz", "rot", "outs", "arr0", "arr1", "arr2", "snt0", "snt1", "snt2"]
 FEET = {}
 
 
@@ -109,7 +111,7 @@ def rank_program(g, core, T, topo):
     def op(q, fn, rd, wr, adds=False, kind=None):
         rd, wr, s = feet(rd), feet(wr), own[q]
         n = cnt.get(s, 0)
-        wait(q, need(q, rd, [] if adds else wr) + ([(s, n)] if q == "p" and n else []) + (across[-1:] if q == "v" and not kind else []))
+        wait(q, need(q, rd, [] if adds else wr) + ([(s, n)] if q == "p" and n and OPT.get("pw") else []) + (across[-1:] if q == "v" and not kind else []))
         cnt[s] = n + 1
         tok = (s, n + 1)
         if kind == "across":
@@ -130,6 +132,11 @@ def rank_program(g, core, T, topo):
             snap[tok] = {k: max(c.get(k, 0) for c, i, o in done) for c, i, o in done for k in c}
             for c, i, o in done:
                 note(tok, i, o)
+
+    def follow(text, **chains):
+        for k in text:
+            next(chains[k], None)
+        weave(*chains.values())
 
     def weave(*chains):
         chains = list(chains)
@@ -184,6 +191,12 @@ def rank_program(g, core, T, topo):
         else:
             op("a", lambda: S.activation(o[0], i[0], AF.Copy, scale=scale), [i], [o])
 
+    def line(o, i, k, c):
+        if OPT.get("line", 1):
+            op("a", lambda: S.activation(o[0], i[0], AF.Identity, bias=a_(c), scale=k), [i, c], [o])
+        else:
+            ts(o, i, k, A.mult, c, A.add)
+
     def fill(o, c):
         op("v", lambda: V.memset(o[0], c), [], [o])
 
@@ -200,79 +213,96 @@ def rank_program(g, core, T, topo):
         op("p", lambda: g.affine_select(o[0], o[0], pattern, k, c, base, step), [o], [o])
 
     dmas("du", [("s", X("ut"), hbm(T.u[:]))])
-    dmas("dx0", [("a", X("xt", s_[:, 0:640]), hbm(T.x[:, 0:640]))])
+    dmas("dx0", [(OPT.get("xq", "s"), X("xt", s_[:, 0:640]), hbm(T.x[:, 0:640]))])
     dmas("dx1", [("s", X("xt", s_[:, 640:1280]), hbm(T.x[:, 640:1280]))])
-    dmas("dw", [("s", raw(X("wq")), hbm(T.wc[:])), ("s", X("wsc"), hbm(T.ws[:]))])
-    dmas("dv", [("s", X("vt"), hbm(T.v[:]))])
+    if OPT.get("wl", 0) == 0:
+        dmas("dw", [("s", raw(X("wq")), hbm(T.wc[:])), ("s", X("wsc"), hbm(T.ws[:]))])
 
     fill(X("et"), 0.0)
+    fill(X("hu"), 0.0)
     iota(X("ti"), [[-32, 4], [0, 2], [7, 2]], 128, 1, True)
-    iota(X("ul"), [[16, 8]], 0, 0)
+
+    def lay(name, idx, c):
+        o = X(name, idx)
+        z = X("hu", s_[:, 0:bin(o[1][0][2]).count("1")])
+        op("a", lambda: S.activation(o[0], z[0], AF.Identity, bias=c), [z], [o])
+
     for k in range(2):
-        fill(X("tb", s_[:, k::2]), 7680.0 + 1280.0 * k)
+        lay("tb", s_[:, k::2], 7680.0 + 1280.0 * k)
+    lay("rst", s_[:], 0.0)
+    iota(X("ul"), [[16, 8]], 0, 0)
     for lo, hi in ((0, 128), (128, EC)):
         select(X("et", s_[:, 4 * lo + 3:4 * hi:4]), [[-1, hi - lo]], A.not_equal, 64.0, 0, 1)
     iota(X("tr"), [[1, 4], [4, 32]], 0, -4)
+    lay("lm", s_[:, 512:1024], 1.0)
+    lay("rst", s_[:, 0:160:16], -BIG)
+    lay("lm", s_[:, 0:512], 1.0)
+
     ts(X("pa"), X("ti", s_[:, 1:2]), 7, A.bitwise_and)
     ts(X("tj"), X("ti", s_[:, 0:16:2]), 5, A.arith_shift_right, 3, A.bitwise_and)
     ts(X("pc"), X("ti", s_[:, 0:1]), 3, A.arith_shift_right, 1, A.bitwise_and)
-    fill(X("rst"), 0.0)
+    ts(X("pd"), X("ti", s_[:, 0:1]), 5, A.arith_shift_right)
+    ts(X("pb"), X("ti", s_[:, 0:1]), 4, A.arith_shift_right, 1, A.bitwise_and)
     copy(X("pm"), X("pa"))
     ts(X("tc"), X("tj"), -2560.0, A.mult)
     copy(X("ph"), X("pc"))
-    fill(X("rst", s_[:, 0:160:16]), -BIG)
-    ts(X("uo"), X("ul"), X("pm"), A.add)
+    ts(X("pt"), X("pd"), -127.0, A.mult, 508.0, A.add)
+    ts(X("cc"), X("pb"), -10240.0, A.mult, 40960.0 - 7 * 8960.0, A.add)
     tt(X("td"), X("tc"), X("tb"), A.add)
-    fill(X("hu"), 0.0)
+
+    def unpacker(b):
+        quant(Q("eq", EC * b, EC * b + EC), X("et", s_[:, 3 - b:3 - b + 4 * EC]))
+
+    ts(X("uo"), X("ul"), X("pm"), A.add)
+    unpacker(0)
     ts(X("te"), X("td"), X("ph"), A.mult)
-    for k in range(2):
-        op("a", lambda: S.activation(T.lm[:, 512 * k:512 * k + 512], T.hu[:, 0:512], AF.Identity, bias=1.0), [X("hu", s_[:, 0:512])], [X("lm", s_[:, 512 * k:512 * k + 512])])
-    for c in range(8):
-        act(X("win", s_[:, 320 * c:320 * c + 320]), X("lm", s_[:, 512:832]), bias=X("te", s_[:, c:c + 1]))
-    for k in (160, 328):
-        fill(X("fm", s_[:, k:k + 8]), 0.0)
-    fill(X("c320"), 320.0)
-    for k, c in ((9, WHOLE), (10, -WHOLE), (11, 149.0)):
-        fill(X("gb", s_[:, k::12]), c)
+    dmas("dq", [("s", X("tq"), X("te", s_[0:128:8, :]))])
+    dmas("dz", [("s", X("win", s_[:, 512 * k:512 * k + 512]), X("lm", s_[:, 512:1024])) for k in range(5)])
+    for b in range(1, OPT.get("e0", 0)):
+        unpacker(b)
     quant(Q("uq", 0, 128), X("ut"))
-    ts(X("pd"), X("ti", s_[:, 0:1]), 5, A.arith_shift_right)
-    ts(X("pb"), X("ti", s_[:, 0:1]), 4, A.arith_shift_right, 1, A.bitwise_and)
+    unpacker(OPT.get("e0", 0))
     words = lambda x: (x[0].bitcast(dt.uint32), x[1])
     copy(words(X("u2")), by(words(X("uq")), X("uo")))
-    copy(X("u2s"), by(X("us"), X("uo")))
+    act(X("u2s"), by(X("us"), X("uo")))
+    for k in (160, 328):
+        lay("fm", s_[:, k:k + 8], 0.0)
+    lay("c320", s_[:], 320.0)
+    for k, c in ((10, WHOLE), (11, -WHOLE), (12, 7.95)):
+        lay("gb", s_[:, k::TERMS], c)
+    lay("of", s_[:, 0:10], 7 * STEP + 8.0)
+    lay("nf", s_[:, 0:10], -7 * STEP - 8.0)
+    act(X("win0"), X("lm", s_[:, 512:832]), bias=X("tq"))
     iota(X("val"), [[0, 4], [32, 5], [1, 16]], 0, 0)
     iota(X("va1"), [[0, 4], [32, 5], [1, 16]], 16, 0)
-    iota(X("va2"), [[1280, 2], [640, 2], [0, 80]], 0, 0)
-    iota(X("mk8"), [[0, 20], [30000, 8]], 0, 0)
-    iota(X("mg"), [[0, 240]], 1, 0)
-    for k, c in ((0, 0), (11, -319)):
-        iota(X("mg", s_[:, k::12]), [[0, 20]], c, 0)
+    iota(X("va2"), [[1280, 2], [160, 2], [0, 80]], 0, 0)
+    iota(X("mk8"), [[1, 2], [0, 10], [30000, 8]], 8 - 2560, 0)
+    iota(X("mg"), [[0, 20 * TERMS]], 1, 0)
+    for k, c in ((0, 0.0), (8, -1.0), (10, -1.00001 / 16), (12, -15.95)):
+        select(X("mg", s_[:, k::TERMS]), [[0, 20]], A.is_gt, c, 0, 0)
     iota(X("mk4"), [[0, 40], [30000, 4]], 0, 0)
     iota(X("nn"), [[0, 32]], 0, 0)
 
     def constants():
-        ts(X("pt"), X("pd"), -127.0, A.mult, 508.0, A.add)
-        for b in range(4):
-            quant(Q("eq", EC * b, EC * b + EC), X("et", s_[:, 3 - b:3 - b + 4 * EC]))
-            if b == 2:
-                ts(X("lm", s_[:, 0:512:4]), X("tr"), X("pt"), A.is_gt)
-            if b:
-                yield
-        yield
+        ts(X("lm", s_[:, 0:512:4]), X("tr"), X("pt"), A.is_gt)
+        for b in range(OPT.get("e0", 0) + 1, 4):
+            unpacker(b)
+            yield
+        lay_lists()
+        window_early()
+        dmas("dl", [("s", X("win", s_[0:128:8, :]), X("win0"))])
         quant(Q("lq", 0, 256), X("lm"))
-        ts(X("cc"), X("pb"), -10240.0, A.mult, 40960.0 - 7 * 8960.0, A.add)
         yield
 
     def lay_lists():
-        dmas("dl", [("s", X("win0", s_[0:16, :]), X("win", s_[0:128:8, :])),
-                    ("s", X("val", s_[16:128:32, :]), X("va1", s_[0:4, :])), ("s", X("val", s_[8:128:16, :]), X("va2", s_[0:8, :]))])
+        dmas("dl", [("s", X("val", s_[16:128:32, :]), X("va1", s_[0:4, :])), ("s", X("val", s_[8:128:16, :]), X("va2", s_[0:8, :]))], False)
 
     CC = X("cc")
 
     def xh(h):
         return Q("xq", 160 * h, 160 * h + 160)
 
-    def choose(h, beside=None):
+    def choose(h, beside=None, after=None):
         n, m, lo = slice(10 * h, 10 * h + 10), slice(5 * h, 5 * h + 5), 160 * h
         quant(xh(h), X("xt", s_[:, 640 * h:640 * h + 640]))
         p = mm(2 * h, 160, Q("u2", 0, 128), xh(h))
@@ -290,82 +320,79 @@ def rank_program(g, core, T, topo):
         yield
         for k in range(4):
             o = 32 * (8 + 5 * h + k) + k
-            tt(X("hu", s_[:, o:o + 160:4]), X("gs", s_[:, m, 1:9]), X("gs", s_[:, m, 0:8]), A.subtract)
+            if k == OPT.get("hs", 9) and not h:
+                yield
+            if k and after:
+                act(X("hu", s_[:, o:o + 160:4]), X("hu", s_[:, 256:416:4]))
+            else:
+                tt(X("hu", s_[:, o:o + 160:4]), X("gs", s_[:, m, 1:9]), X("gs", s_[:, m, 0:8]), A.subtract)
+        if after:
+            after()
         yield
 
-    def unpack(d, h):
-        for b in range(4):
-            e, o = EC * b + 16 * d, 1280 * (d + 1) + 640 * h + 160 * b
-            act(X("tw", s_[:, o:o + 160]), mm(bank(), 160, Q("eq", e, e + 128), xh(h)), 0.015625)
+    def unpack(d, bs=range(4)):
+        for b in bs:
+            e, o = EC * b + 16 * d, 1280 * (d + 1) + 320 * b
+            act(X("tw", s_[:, o:o + 320]), mm(bank(), 320, Q("eq", e, e + 128), Q("xq", 0, 320)), 0.015625)
 
-    def turn(ds, h, close=False):
-        jobs = []
-        for d in ds:
-            o = 1280 * (d + 1) + 640 * h
-            for to in [o + 5120] + [640 * h] * (d == 3):
-                jobs += [("s", X("tw", s_[64 * k:64 * k + 64, to:to + 640]), X("tw", s_[64 - 64 * k:128 - 64 * k, o:o + 640])) for k in range(2)]
-            if OPT.get("dup") and d < 2:
-                jobs += [("s", X("tw2", s_[64 * k:64 * k + 64, 640 * d:640 * d + 640]), X("tw", s_[64 - 64 * k:128 - 64 * k, o:o + 640])) for k in range(2)]
-        dmas("rot", jobs, close)
+    def turn(d, close=False):
+        o = 1280 * (d + 1)
+        dmas("rot", [("s", X("tw", s_[64 * k:64 * k + 64, to:to + 1280]), X("tw", s_[64 - 64 * k:128 - 64 * k, o:o + 1280]))
+                     for to in [o + 5120] + [0] * (d == 3) for k in range(2)], close)
 
     def window_early():
-        unpack(0, 0)
-        unpack(1, 0)
-        turn((0, 1), 0)
+        unpack(3)
+        turn(3)
+        unpack(2, range(OPT.get("we", 4)))
 
-    def window_mid():
-        unpack(3, 1)
-        unpack(2, 1)
-        turn((3, 2), 1)
-
-    def window_late():
-        unpack(3, 0)
-        unpack(2, 0)
-        if 4 in OPT["pe"]:
-            turn((3, 2), 0, True)
-            for d in (0, 1, 4, 5) + OPT.get("more", ()):
-                unpack(d, 1)
-        else:
-            turn((3, 2), 0)
-            unpack(0, 1)
-            unpack(1, 1)
-            turn((0, 1), 1, True)
+    def window_rest():
+        n, k = OPT.get("we", 4), OPT.get("wr", 1)
+        steps = [(2, b) for b in range(n, 4)] + [(d, b) for d in OPT["pe"] for b in range(4)]
+        if n == 4:
+            turn(2)
+        for i, (d, b) in enumerate(steps):
+            if i == k:
+                yield
+            unpack(d, [b])
+            if b == 3 and d < 4 and d + 4 not in OPT["pe"]:
+                turn(d, d == OPT["last"])
 
     def places(t):
         lo = 64 if t else 0
+        for e in range(2):
+            ts(X("dd", s_[:, 80 * e:80 * e + 80]), X("gg", s_[:, e:20:2, 0:8]), -STEP - FAR, A.mult, FAR, A.add)
         quant(Q("hq", lo, 192), X("hu", s_[:, 4 * lo:768]))
         for k in range(3):
             mm(1, 128, Q("lq", 128 * min(k, 1), 128 * min(k, 1) + 128), Q("hq", 64 - 32 * k, 192 - 32 * k), k == 0, k == 2)
-        if t == 0:
-            window_mid()
-            fill(X("mg", s_[:, 9::12]), 1.0 / 320)
-        window_late()
         A0 = X("p1", s_[:, 0:80])
-        tt(X("h0"), X("gg", s_[:, 0:20:2, 1:9]), X("gg", s_[:, 0:20:2, 0:8]), A.subtract)
-        for e in range(2):
-            ts(X("dd", s_[:, 80 * e:80 * e + 80]), X("gg", s_[:, e:20:2, 0:8]), -STEP - FAR, A.mult, FAR, A.add)
-        scan(X("th"), X("dd"), X("c320"), 0.0, A.add, A.min)
-        tt(X("a1"), A0, X("h0"), A.add)
-        ts(X("occ"), X("p1", s_[:, 80:88]), 320.0, A.min)
-        ts(X("rl", s_[:, 0:80]), A0, 320.0, A.max, 8.5 / 8 - 320.0, A.add)
-        scan(X("pk", s_[:, 0:80]), X("dd", s_[:, 0:80]), A0, 0.0, A.add, A.min)
-        ts(X("rl", s_[:, 80:160]), X("a1"), 320.0, A.max, 8.5 / 8 - 320.0, A.add)
-        scan(X("pk", s_[:, 80:160]), X("dd", s_[:, 80:160]), X("a1"), 0.0, A.add, A.min)
-        scan(X("fb"), X("c320", s_[:, 0:8]), X("occ"), 8.5, A.add, A.subtract)
-        ts(X("wv"), X("occ"), STEP - 320.0, A.add, 20.0, A.mult)
-        scan(X("rs"), X("mk8"), X("rl"), 0.0, A.min, A.add)
         F, TH, R = X("pk", s_[:, 7:160:8]), X("th", s_[:, 7:160:8]), X("rs", s_[:, 7:160:8])
-        tt(X("ac"), F, TH, A.is_lt)
-        ts(X("fp"), F, 7 * STEP + 8.5, A.add, 20.0, A.mult)
-        tt(X("mg", s_[:, 8:240:12]), F, TH, A.is_ge)
-        ts(X("gb", s_[:, 0:240:12]), R, X("occ", s_[:, 0:1]), A.add, 20.0, A.mult)
+        tt(X("h0"), X("gg", s_[:, 0:20:2, 0:8]), X("gg", s_[:, 0:20:2, 1:9]), A.subtract)
+        scan(X("th"), X("dd"), X("c320"), 0.0, A.add, A.min)
+        ts(X("h1"), X("h0"), 320.0, A.add)
+        tt(X("same"), X("th", s_[:, 7:80:8]), X("th", s_[:, 87:160:8]), A.is_equal)
+        line(X("of", s_[:, 10:20]), X("same"), 1.0, 7 * STEP + 8.0)
+        line(X("nf", s_[:, 10:20]), X("same"), -1.0, -7 * STEP - 8.0)
+        ts(X("occ"), X("p1", s_[:, 80:88]), 320.0, A.min)
+        line(X("wv"), X("occ"), 1.0, STEP - 320.0)
+        rest = window_rest()
+        next(rest)
+        tt(X("rl", s_[:, 80:160]), A0, X("h1"), A.max)
+        ts(X("rl", s_[:, 0:80]), A0, 320.0, A.max)
+        tt(X("th", s_[:, 87:160:8]), X("th", s_[:, 87:160:8]), X("same"), A.subtract)
+        for e in range(2):
+            scan(X("pk", s_[:, 80 * e:80 * e + 80]), X("dd", s_[:, 80 * e:80 * e + 80]), A0, 0.0, A.add, A.min)
+        scan(X("fb"), X("c320", s_[:, 0:8]), X("occ"), 8.0, A.add, A.subtract)
+        scan(X("rs"), X("mk8"), X("rl"), 0.0, A.min, A.add)
+        tt(X("mg", s_[:, 9::TERMS]), F, TH, A.is_ge)
+        tt(X("gb", s_[:, 8::TERMS]), F, X("of"), A.add)
+        tt(X("gb", s_[:, 9::TERMS]), X("nf"), F, A.subtract)
+        line(X("gb", s_[:, 0::TERMS]), R, 1.0, X("occ", s_[:, 0:1]))
+        weave(rest)
         for c in range(1, 8):
-            if c == 4:
-                tt(X("gb", s_[:, 8:240:12]), X("fp"), X("ac"), A.mult)
-            ts(X("gb", s_[:, c:240:12]), R, X("fb", s_[:, c - 1:c]), A.is_ge, X("wv", s_[:, c:c + 1]), A.mult)
+            ts(X("gb", s_[:, c::TERMS]), R, X("fb", s_[:, c - 1:c]), A.is_ge, X("wv", s_[:, c:c + 1]), A.mult)
         scan(X("gt"), X("mg"), X("gb"), 0.0, A.mult, A.add)
-        tt(X("z3"), X("gt", s_[:, 8:240:12]), X("gt", s_[:, 11:240:12]), A.add)
-        copy(X("sl"), X("z3"))
+        tt(X("z3"), X("gt", s_[:, 12::TERMS]), X("gt", s_[:, 9::TERMS]), A.subtract)
+        ts(X("sl"), X("z3"), 20.0, A.mult)
         op("v", lambda: V.tensor_copy(T.win[:].indirect(T.sl[:]), T.val[:]), [X("sl"), X("val")], [X("win")])
 
     def turns(ks):
@@ -385,12 +412,14 @@ def rank_program(g, core, T, topo):
         yield
         for b in (0, 2, 1, 3):
             o = X("yt", s_[:, 640 * h + b:640 * h + 640:4])
-            i = by(X("tw", s_[:, 160 * b:160 * b + 11040]), X("gl", s_[:, 10 * h:10 * h + 10]))
-            if b < 2:
+            i = by(X("tw", s_[:, 320 * b:320 * b + 10560]), X("gl", s_[:, 10 * h:10 * h + 10]))
+            if b < OPT.get("gv", (2, 2))[h]:
                 copy(o, i)
             else:
                 act(o, i)
         yield
+        for k in range(OPT.get("gy", 0) * h):
+            yield
 
     def cross(t):
         yield from sources(1)
@@ -403,19 +432,26 @@ def rank_program(g, core, T, topo):
             mask |= 1 << e
         wait("p", need("p", feet(out), []))
         arr, snt = T.sem["arr%d" % t], T.sem["snt%d" % t]
-        g.remote_dma(raw(land[0])[0], raw(out[0])[0], arr, snt, pid, rid, mask)
-        g.remote_dma(land[1][0], out[1][0], arr, snt, pid, rid, mask)
+        free = topo.engines(core, dst)
+        if len(free) >= 16 and OPT.get("fuse"):
+            sides = [(raw(X("lc%d" % t, s_[:, 40 * k:40 * k + 40]))[0], raw(X("ac%d" % t, s_[:, 40 * k:40 * k + 40]))[0]) for k in range(4)] + [(land[1][0], out[1][0])]
+            cuts = [0, 4, 8, 12, 14, 16]
+            g.remote_dma_fused([RemoteDMATransfer(dst_ids=[DstId(rid=rid, pnc=pid)], dma_engine_mask=sum(1 << e for e in free[cuts[k]:cuts[k + 1]]),
+                                                  remote_sem=arr, src=i, dst=o) for k, (o, i) in enumerate(sides)], local_sem=snt)
+        else:
+            g.remote_dma(raw(land[0])[0], raw(out[0])[0], arr, snt, pid, rid, mask)
+            g.remote_dma(land[1][0], out[1][0], arr, snt, pid, rid, mask)
         snap[("arr%d" % t, 16)] = {}
         note(("arr%d" % t, 16), [], feet(land))
         cnt["arr%d" % t] = cnt["snt%d" % t] = 16
         yield
 
     def stay_list(t):
-        for ks in ((0, 1, 2, 3), (4, 5, 6, 7), (8, 9)):
+        for ks in OPT.get("tk", ((), (0, 1, 2, 3), (4, 5, 6, 7), (8, 9)))[1:]:
             turns(ks)
             yield
         if t < 2:
-            dmas("dz", [("s", X("win", s_[0:128:8, :]), X("win0", s_[0:16, :]))])
+            dmas("dz", [("s", X("win", s_[0:128:8, :]), X("win0"))])
         yield from sources(0)
 
     def layer_stay():
@@ -430,19 +466,24 @@ def rank_program(g, core, T, topo):
             act(X("xt", s_[:, b:640:4]), X("t64", s_[:, 160 * b:160 * b + 160]), 0.015625)
         yield
 
+    def for_the_end():
+        ts(X("pd"), X("ti", s_[:, 0:1]), 4, A.arith_shift_right)
+        ts(X("c4"), CC, -160.0, A.add)
+        yield
+        quant(Q("vq", 0, 128), X("vt"))
+        ts(X("ph"), X("pd"), 7.0, A.add)
+        yield
+
     def numbers():
         ts(X("gi"), X("w3"), X("c4"), A.add, 0.00078125, A.mult)
-        ts(X("mi"), X("w3"), X("c8"), A.add, 0.0015625, A.mult)
         ts(X("n2"), X("w3"), CC, A.add, 8.0, A.mult)
         yield
         ts(X("gj"), X("gi"), X("ph"), A.add)
-        ts(X("n3"), X("mi"), -3840.0, A.mult)
-        ts(X("n4"), X("gi"), -2560.0, A.mult)
+        ts(X("n4"), X("gi"), -10240.0, A.mult)
         ts(X("gk"), X("gj"), 7, A.bitwise_and)
-        tt(X("n5"), X("n2"), X("n3"), A.add)
-        tt(X("n6"), X("gk"), X("n4"), A.add)
+        tt(X("n5"), X("n2"), X("n4"), A.add)
         yield
-        tt(X("nn", s_[:, 0:20]), X("n6"), X("n5"), A.add)
+        tt(X("nn", s_[:, 0:20]), X("gk"), X("n5"), A.add)
         yield
         turn32(X("omt"), X("nn"))
         dmas("outs", [("s", hbm(T.om[c:c + 1, :]), X("omt", s_[32 * (c // 2):32 * (c // 2) + 20, 16 * (c % 2):16 * (c % 2) + 16])) for c in range(8)], False)
@@ -455,7 +496,7 @@ def rank_program(g, core, T, topo):
             mm(k, 160, Q("wq", 128 * b, 128 * b + 128), land, True, False)
             p = mm(k, 160, Q("eq", EC * b, EC * b + 128), land, False, True)
             o = X("xt", s_[:, 640 + b:1280:4])
-            if t == 2 and b % 2 == 0:
+            if b in OPT["ev"][t]:
                 ts(o, p, 0.015625, A.mult)
             else:
                 act(o, p, 0.015625)
@@ -465,27 +506,20 @@ def rank_program(g, core, T, topo):
             yield
         yield from chain
 
-    weave(choose(0), choose(1), constants())
-    lay_lists()
-    window_early()
+    follow(OPT["or0"], k=choose(0), r=choose(1), c=constants())
     for t in range(3):
         places(t)
-        turns(range(10, 20))
-        weave(cross(t), stay_list(t))
-        weave(layer_stay(), numbers() if t == 2 else iter(()))
         if t == 0:
-            quant(Q("vq", 0, 128), X("vt"))
-            ts(X("pd"), X("ti", s_[:, 0:1]), 4, A.arith_shift_right)
-            ts(X("c4"), CC, -400.0, A.add)
-            ts(X("c8"), CC, -80.0, A.add)
-            ts(X("ph"), X("pd"), 7.0, A.add)
-        if t < 2 and t in OPT["rfirst"]:
+            if OPT.get("wl", 0) == 1:
+                dmas("dw", [("s", raw(X("wq")), hbm(T.wc[:])), ("s", X("wsc"), hbm(T.ws[:]))])
+            dmas("dv", [("s", X("vt"), hbm(T.v[:]))])
+        turns(range(10, 20))
+        turns(OPT.get("tk", ((), (0, 1, 2, 3), (4, 5, 6, 7), (8, 9)))[0])
+        weave(cross(t), stay_list(t))
+        weave(layer_stay(), numbers() if t == 2 else for_the_end() if t == 0 else iter(()))
+        if t < 2:
             layer_arrived(t)
-            weave(choose(0), later(OPT.get("lag", 1), choose(1, lambda: (window_early(), window_mid()))))
-        elif t < 2:
-            weave(choose(0, window_early))
-            layer_arrived(t)
-            weave(choose(1, window_mid))
+            follow(OPT["ord"][t], k=choose(0), r=choose(1, window_early))
 
     quant(xh(0), X("xt", s_[:, 0:640]))
     layer_arrived(2)

import numpy as np
from concourse.bass import DstId, RemoteDMATransfer
from concourse.mybir import dt, AluOpType as A, ActivationFunctionType as AF

ROUNDS = [1, 2, 4]
BIG = float(2.0 ** 75)
FAR = 65536.0
STEP = 5120.0
WHOLE = 12582912.0
TERMS = 13
EC = 192
SCRATCH = {}
OPT = {"lag": (1, 0), "we": 2, "ev": ((), (0, 1), (0, 2)), "ord": ("kkrkkrkrkr", "krkkrkrkrkrk"), "or0": "krckrkrkrkcrk", "hs": 2, "wl": 1, "e0": 2, "tk": ((0, 1, 2), (3, 4, 5), (6, 7, 8, 9), ()), "pe": (1, 0, 4), "last": 1}


def _declare(where, dtype, text):
    for item in text.split():
        name, dims = item.split(":")
        SCRATCH[name] = (where, [128] + [int(k) for k in dims.split("x")], dtype)


_declare("sbuf", "bfloat16", "xt:1280 yt:1280 y64:640 ut:512 vt:512 et:%d lm:1024 hu:768 tw:11520 tw2:1280 gg:20x16 gs:10x9 h0:80 dd:160 "
         "c320:160 mk4:160 val:320 va1:320 va2:320 win:2560 win0:320 wt:2560" % (4 * EC + 8))
_declare("sbuf", "float32", "st:320 fm:336 rst:160 pk:160 th:160 mk8:160 wv:8 z3:20 h1:80 same:10 of:20 nf:20 rl:160 rs:160 occ:8 fb:8 gb:260 gt:260 mg:260 "
         "s4:320 u1:80 w3:20 cc:1 c4:1 c8:1 pm:1 ph:1 pt:1 tq:1 tr:128 ul:8 tb:8 tc:8 td:8 te:8 n1:20 n2:20 n3:20 n4:20 n5:20 n6:20 nn:32 omt:32 yo:320 t64:640")
_declare("sbuf", "int32", "pa:1 pb:1 pc:1 pd:1 ti:16 tj:8 gi:20 mi:20 gj:20 gk:20")
_declare("sbuf", "uint16", "sl:20 gl:20 uo:8")
PAIRS = [("xq", "xs", 320), ("uq", "us", 128), ("u2", "u2s", 128), ("vq", "vs", 128), ("wq", "wsc", 512), ("eq", "es", 4 * EC), ("lq", "lqs", 256),
         ("hq", "hs", 192), ("zq", "zs", 160)] + [(_k + "c%d" % _t, _k + "s%d" % _t, 160) for _t in range(3) for _k in "al"]
for _n, _s, _w in PAIRS:
    SCRATCH[_n] = ("sbuf", [128, _w], "float8_e4m3fn_x4")
    SCRATCH[_s] = ("sbuf", [128, _w], "uint8")
PLANE = {_n: _s for _n, _s, _w in PAIRS}
for _t in range(8):
    SCRATCH["p%d" % _t] = ("psum", [128, 512], "float32")
SEMAPHORES = ["qv", "qt", "qa", "qp", "dx0", "dx1", "du", "dv", "dw", "dl", "dq", "dz", "rot", "outs", "arr0", "arr1", "arr2", "snt0", "snt1", "snt2"]
FEET = {}


def _foot(name, idx):
    key = (name, repr(idx))
    if key not in FEET:
        m = np.zeros(SCRATCH[name][1], bool)
        m[idx] = True
        m = m.reshape(128, -1)
        if SCRATCH[name][0] == "psum":
            m[:] = True
        FEET[key] = (name,) + tuple(int.from_bytes(np.packbits(k).tobytes(), "big") for k in (m.any(axis=1), m.any(axis=0)))
    return FEET[key]


def rank_program(g, core, T, topo):
    rank = T.rank_of(core)
    if rank is None:
        return
    V, P, S, Y = g.vector, g.tensor, g.scalar, g.sync
    s_ = np.s_
    queue = {"v": V, "t": P, "a": S, "s": Y, "p": g}
    own = {"v": "qv", "t": "qt", "a": "qa", "p": "qp"}
    cnt, clock, snap = {}, {q: {} for q in queue}, {}
    wrote, read, pending = {}, {}, {}

    def X(name, idx=s_[:]):
        return (T[name][idx], [_foot(name, idx)])

    def Q(name, lo, hi):
        return X(name, s_[:, lo:hi]), X(PLANE[name], s_[:, lo:hi])

    def by(win, off):
        return (win[0].indirect(off[0]), win[1] + off[1])

    def meet(a, b):
        return a[1] & b[1] and a[2] & b[2]

    def need(q, rd, wr):
        d = []
        for r in rd:
            d += [t for (x, t) in wrote.get(r[0], []) if meet(r, x)]
            if SCRATCH[r[0]][0] == "psum":
                d += [t for (x, t) in read.get(r[0], []) if t[0] != own[q]]
        for r in wr:
            d += [t for (x, t) in wrote.get(r[0], []) + read.get(r[0], []) if meet(r, x)]
        return d

    def wait(q, toks):
        top = {}
        for s, v in toks:
            top[s] = max(top.get(s, 0), v)
        for s in list(top):
            implied = any(o != s and snap[(o, top[o])].get(s, 0) >= top[s] for o in top)
            if not implied and clock[q].get(s, 0) < top[s]:
                queue[q].wait_ge(T.sem[s], top[s])
        for s, v in top.items():
            for o, w in snap[(s, v)].items():
                clock[q][o] = max(clock[q].get(o, 0), w)
            clock[q][s] = max(clock[q].get(s, 0), v)

    def note(tok, rd, wr):
        for r in wr:
            for tab in (wrote, read):
                tab[r[0]] = [(x, t) for (x, t) in tab.get(r[0], []) if x[1] & ~r[1] or x[2] & ~r[2]]
            wrote[r[0]].append((r, tok))
        for r in rd:
            read.setdefault(r[0], []).append((r, tok))

    def feet(l):
        return [f for x in l if isinstance(x, tuple) for f in x[1]]

    across = []

    def op(q, fn, rd, wr, adds=False, kind=None):
        rd, wr, s = feet(rd), feet(wr), own[q]
        n = cnt.get(s, 0)
        wait(q, need(q, rd, [] if adds else wr) + ([(s, n)] if q == "p" and n and OPT.get("pw") else []) + (across[-1:] if q == "v" and not kind else []))
        cnt[s] = n + 1
        tok = (s, n + 1)
        if kind == "across":
            across.append(tok)
        snap[tok] = dict(clock[q])
        fn().then_inc(T.sem[s], 1)
        note(tok, rd, wr)

    def dmas(s, jobs, close=True):
        for q, o, i in jobs:
            wait(q, need(q, i[1], o[1]))
            queue[q].dma_start(o[0], i[0]).then_inc(T.sem[s], 16)
            pending.setdefault(s, []).append((dict(clock[q]), i[1], o[1]))
        if close:
            done = pending.pop(s)
            cnt[s] = cnt.get(s, 0) + 16 * len(done)
            tok = (s, cnt[s])
            snap[tok] = {k: max(c.get(k, 0) for c, i, o in done) for c, i, o in done for k in c}
            for c, i, o in done:
                note(tok, i, o)

    def follow(text, **chains):
        for k in text:
            next(chains[k], None)
        weave(*chains.values())

    def weave(*chains):
        chains = list(chains)
        while chains:
            for c in list(chains):
                if next(c, "end") == "end":
                    chains.remove(c)

    def hbm(ap):
        return (ap, [])

    def raw(x):
        return (x[0].bitcast(dt.uint8), x[1])

    def a_(x):
        return x[0] if isinstance(x, tuple) else x

    def mm(bank, n, lhs, rhs, start=True, stop=True):
        out = X("p%d" % bank, s_[:, 0:n])
        op("t", lambda: P.matmul_mx(out[0], lhs[0][0], lhs[1][0], rhs[0][0], rhs[1][0], start, stop), list(lhs + rhs), [out], not start)
        return out

    pool = [0]

    def bank():
        pool[0] += 1
        return 3 + pool[0] % 5

    def tt(o, a, b, k):
        op("v", lambda: V.tensor_tensor(o[0], a[0], b[0], k), [a, b], [o], kind="across" if a[1][0][1] != b[1][0][1] else None)

    def ts(o, a, s1, k0, s2=None, k1=None):
        if k1 is None:
            op("v", lambda: V.tensor_scalar(o[0], a[0], a_(s1), None, k0), [a, s1], [o])
        else:
            op("v", lambda: V.tensor_scalar(o[0], a[0], a_(s1), a_(s2), k0, k1), [a, s1, s2], [o])

    def scan(o, a, b, first, k0, k1):
        op("v", lambda: V.tensor_tensor_scan(o[0], a[0], b[0], first, k0, k1), [a, b], [o])

    def copy(o, i):
        op("v", lambda: V.tensor_copy(o[0], i[0]), [i], [o])

    def turn32(o, i):
        op("v", lambda: V.transpose(o[0], i[0]), [i], [o], kind="turn")

    def act(o, i, scale=None, bias=None):
        if bias is not None:
            op("a", lambda: S.activation(o[0], i[0], AF.Identity, bias=bias[0], scale=0.0), [i, bias], [o])
        elif scale is None:
            op("a", lambda: S.activation(o[0], i[0], AF.Copy), [i], [o])
        else:
            op("a", lambda: S.activation(o[0], i[0], AF.Copy, scale=scale), [i], [o])

    def line(o, i, k, c):
        if OPT.get("line", 1):
            op("a", lambda: S.activation(o[0], i[0], AF.Identity, bias=a_(c), scale=k), [i, c], [o])
        else:
            ts(o, i, k, A.mult, c, A.add)

    def fill(o, c):
        op("v", lambda: V.memset(o[0], c), [], [o])

    def quant(q, i):
        op("v", lambda: V.quantize_mx(q[0][0], q[1][0], i[0]), [i], list(q))

    def iota(o, pattern, base, step, whole=False):
        if whole:
            op("p", lambda: g.iota(o[0], pattern, base, step), [], [o])
        else:
            op("p", lambda: g.iota(o[0], pattern, base, step, allow_small_or_imprecise_dtypes=True), [], [o])

    def select(o, pattern, k, c, base, step):
        op("p", lambda: g.affine_select(o[0], o[0], pattern, k, c, base, step), [o], [o])

    dmas("du", [("s", X("ut"), hbm(T.u[:]))])
    dmas("dx0", [(OPT.get("xq", "s"), X("xt", s_[:, 0:640]), hbm(T.x[:, 0:640]))])
    dmas("dx1", [("s", X("xt", s_[:, 640:1280]), hbm(T.x[:, 640:1280]))])
    if OPT.get("wl", 0) == 0:
        dmas("dw", [("s", raw(X("wq")), hbm(T.wc[:])), ("s", X("wsc"), hbm(T.ws[:]))])

    fill(X("et"), 0.0)
    fill(X("hu"), 0.0)
    iota(X("ti"), [[-32, 4], [0, 2], [7, 2]], 128, 1, True)

    def lay(name, idx, c):
        o = X(name, idx)
        z = X("hu", s_[:, 0:bin(o[1][0][2]).count("1")])
        op("a", lambda: S.activation(o[0], z[0], AF.Identity, bias=c), [z], [o])

    for k in range(2):
        lay("tb", s_[:, k::2], 7680.0 + 1280.0 * k)
    lay("rst", s_[:], 0.0)
    iota(X("ul"), [[16, 8]], 0, 0)
    for lo, hi in ((0, 128), (128, EC)):
        select(X("et", s_[:, 4 * lo + 3:4 * hi:4]), [[-1, hi - lo]], A.not_equal, 64.0, 0, 1)
    iota(X("tr"), [[1, 4], [4, 32]], 0, -4)
    lay("lm", s_[:, 512:1024], 1.0)
    lay("rst", s_[:, 0:160:16], -BIG)
    lay("lm", s_[:, 0:512], 1.0)

    ts(X("pa"), X("ti", s_[:, 1:2]), 7, A.bitwise_and)
    ts(X("tj"), X("ti", s_[:, 0:16:2]), 5, A.arith_shift_right, 3, A.bitwise_and)
    ts(X("pc"), X("ti", s_[:, 0:1]), 3, A.arith_shift_right, 1, A.bitwise_and)
    ts(X("pd"), X("ti", s_[:, 0:1]), 5, A.arith_shift_right)
    ts(X("pb"), X("ti", s_[:, 0:1]), 4, A.arith_shift_right, 1, A.bitwise_and)
    copy(X("pm"), X("pa"))
    ts(X("tc"), X("tj"), -2560.0, A.mult)
    copy(X("ph"), X("pc"))
    ts(X("pt"), X("pd"), -127.0, A.mult, 508.0, A.add)
    ts(X("cc"), X("pb"), -10240.0, A.mult, 40960.0 - 7 * 8960.0, A.add)
    tt(X("td"), X("tc"), X("tb"), A.add)

    def unpacker(b):
        quant(Q("eq", EC * b, EC * b + EC), X("et", s_[:, 3 - b:3 - b + 4 * EC]))

    ts(X("uo"), X("ul"), X("pm"), A.add)
    unpacker(0)
    ts(X("te"), X("td"), X("ph"), A.mult)
    dmas("dq", [("s", X("tq"), X("te", s_[0:128:8, :]))])
    dmas("dz", [("s", X("win", s_[:, 512 * k:512 * k + 512]), X("lm", s_[:, 512:1024])) for k in range(5)])
    for b in range(1, OPT.get("e0", 0)):
        unpacker(b)
    quant(Q("uq", 0, 128), X("ut"))
    unpacker(OPT.get("e0", 0))
    words = lambda x: (x[0].bitcast(dt.uint32), x[1])
    copy(words(X("u2")), by(words(X("uq")), X("uo")))
    act(X("u2s"), by(X("us"), X("uo")))
    for k in (160, 328):
        lay("fm", s_[:, k:k + 8], 0.0)
    lay("c320", s_[:], 320.0)
    for k, c in ((10, WHOLE), (11, -WHOLE), (12, 7.95)):
        lay("gb", s_[:, k::TERMS], c)
    lay("of", s_[:, 0:10], 7 * STEP + 8.0)
    lay("nf", s_[:, 0:10], -7 * STEP - 8.0)
    act(X("win0"), X("lm", s_[:, 512:832]), bias=X("tq"))
    iota(X("val"), [[0, 4], [32, 5], [1, 16]], 0, 0)
    iota(X("va1"), [[0, 4], [32, 5], [1, 16]], 16, 0)
    iota(X("va2"), [[1280, 2], [160, 2], [0, 80]], 0, 0)
    iota(X("mk8"), [[1, 2], [0, 10], [30000, 8]], 8 - 2560, 0)
    iota(X("mg"), [[0, 20 * TERMS]], 1, 0)
    for k, c in ((0, 0.0), (8, -1.0), (10, -1.00001 / 16), (12, -15.95)):
        select(X("mg", s_[:, k::TERMS]), [[0, 20]], A.is_gt, c, 0, 0)
    iota(X("mk4"), [[0, 40], [30000, 4]], 0, 0)
    iota(X("nn"), [[0, 32]], 0, 0)

    def constants():
        ts(X("lm", s_[:, 0:512:4]), X("tr"), X("pt"), A.is_gt)
        for b in range(OPT.get("e0", 0) + 1, 4):
            unpacker(b)
            yield
        lay_lists()
        window_early()
        dmas("dl", [("s", X("win", s_[0:128:8, :]), X("win0"))])
        quant(Q("lq", 0, 256), X("lm"))
        yield

    def lay_lists():
        dmas("dl", [("s", X("val", s_[16:128:32, :]), X("va1", s_[0:4, :])), ("s", X("val", s_[8:128:16, :]), X("va2", s_[0:8, :]))], False)

    CC = X("cc")

    def xh(h):
        return Q("xq", 160 * h, 160 * h + 160)

    def choose(h, beside=None, after=None):
        n, m, lo = slice(10 * h, 10 * h + 10), slice(5 * h, 5 * h + 5), 160 * h
        quant(xh(h), X("xt", s_[:, 640 * h:640 * h + 640]))
        p = mm(2 * h, 160, Q("u2", 0, 128), xh(h))
        if beside:
            beside()
        yield
        st, fm = X("st", s_[:, lo:lo + 160]), X("fm", s_[:, 168 * h:168 * h + 160])
        turn32(st, p)
        yield
        scan(fm, st, X("rst"), 0.0, A.max, A.add)
        yield
        tt(X("gg", s_[:, n, :]), fm, X("fm", s_[:, 168 * h + 7:168 * h + 167]), A.is_ge)
        yield
        tt(X("gs", s_[:, m, :]), X("gg", s_[:, 10 * h:10 * h + 10:2, 0:9]), X("gg", s_[:, 10 * h + 1:10 * h + 10:2, 0:9]), A.add)
        yield
        for k in range(4):
            o = 32 * (8 + 5 * h + k) + k
            if k == OPT.get("hs", 9) and not h:
                yield
            if k and after:
                act(X("hu", s_[:, o:o + 160:4]), X("hu", s_[:, 256:416:4]))
            else:
                tt(X("hu", s_[:, o:o + 160:4]), X("gs", s_[:, m, 1:9]), X("gs", s_[:, m, 0:8]), A.subtract)
        if after:
            after()
        yield

    def unpack(d, bs=range(4)):
        for b in bs:
            e, o = EC * b + 16 * d, 1280 * (d + 1) + 320 * b
            act(X("tw", s_[:, o:o + 320]), mm(bank(), 320, Q("eq", e, e + 128), Q("xq", 0, 320)), 0.015625)

    def turn(d, close=False):
        o = 1280 * (d + 1)
        dmas("rot", [("s", X("tw", s_[64 * k:64 * k + 64, to:to + 1280]), X("tw", s_[64 - 64 * k:128 - 64 * k, o:o + 1280]))
                     for to in [o + 5120] + [0] * (d == 3) for k in range(2)], close)

    def window_early():
        unpack(3)
        turn(3)
        unpack(2, range(OPT.get("we", 4)))

    def window_rest():
        n, k = OPT.get("we", 4), OPT.get("wr", 1)
        steps = [(2, b) for b in range(n, 4)] + [(d, b) for d in OPT["pe"] for b in range(4)]
        if n == 4:
            turn(2)
        for i, (d, b) in enumerate(steps):
            if i == k:
                yield
            unpack(d, [b])
            if b == 3 and d < 4 and d + 4 not in OPT["pe"]:
                turn(d, d == OPT["last"])

    def places(t):
        lo = 64 if t else 0
        for e in range(2):
            ts(X("dd", s_[:, 80 * e:80 * e + 80]), X("gg", s_[:, e:20:2, 0:8]), -STEP - FAR, A.mult, FAR, A.add)
        quant(Q("hq", lo, 192), X("hu", s_[:, 4 * lo:768]))
        for k in range(3):
            mm(1, 128, Q("lq", 128 * min(k, 1), 128 * min(k, 1) + 128), Q("hq", 64 - 32 * k, 192 - 32 * k), k == 0, k == 2)
        A0 = X("p1", s_[:, 0:80])
        F, TH, R = X("pk", s_[:, 7:160:8]), X("th", s_[:, 7:160:8]), X("rs", s_[:, 7:160:8])
        tt(X("h0"), X("gg", s_[:, 0:20:2, 0:8]), X("gg", s_[:, 0:20:2, 1:9]), A.subtract)
        scan(X("th"), X("dd"), X("c320"), 0.0, A.add, A.min)
        ts(X("h1"), X("h0"), 320.0, A.add)
        tt(X("same"), X("th", s_[:, 7:80:8]), X("th", s_[:, 87:160:8]), A.is_equal)
        line(X("of", s_[:, 10:20]), X("same"), 1.0, 7 * STEP + 8.0)
        line(X("nf", s_[:, 10:20]), X("same"), -1.0, -7 * STEP - 8.0)
        ts(X("occ"), X("p1", s_[:, 80:88]), 320.0, A.min)
        line(X("wv"), X("occ"), 1.0, STEP - 320.0)
        rest = window_rest()
        next(rest)
        tt(X("rl", s_[:, 80:160]), A0, X("h1"), A.max)
        ts(X("rl", s_[:, 0:80]), A0, 320.0, A.max)
        tt(X("th", s_[:, 87:160:8]), X("th", s_[:, 87:160:8]), X("same"), A.subtract)
        for e in range(2):
            scan(X("pk", s_[:, 80 * e:80 * e + 80]), X("dd", s_[:, 80 * e:80 * e + 80]), A0, 0.0, A.add, A.min)
        scan(X("fb"), X("c320", s_[:, 0:8]), X("occ"), 8.0, A.add, A.subtract)
        scan(X("rs"), X("mk8"), X("rl"), 0.0, A.min, A.add)
        tt(X("mg", s_[:, 9::TERMS]), F, TH, A.is_ge)
        tt(X("gb", s_[:, 8::TERMS]), F, X("of"), A.add)
        tt(X("gb", s_[:, 9::TERMS]), X("nf"), F, A.subtract)
        line(X("gb", s_[:, 0::TERMS]), R, 1.0, X("occ", s_[:, 0:1]))
        weave(rest)
        for c in range(1, 8):
            ts(X("gb", s_[:, c::TERMS]), R, X("fb", s_[:, c - 1:c]), A.is_ge, X("wv", s_[:, c:c + 1]), A.mult)
        scan(X("gt"), X("mg"), X("gb"), 0.0, A.mult, A.add)
        tt(X("z3"), X("gt", s_[:, 12::TERMS]), X("gt", s_[:, 9::TERMS]), A.subtract)
        ts(X("sl"), X("z3"), 20.0, A.mult)
        op("v", lambda: V.tensor_copy(T.win[:].indirect(T.sl[:]), T.val[:]), [X("sl"), X("val")], [X("win")])

    def turns(ks):
        for k in ks:
            turn32(X("wt", s_[:, 128 * k:128 * k + 128]), X("win", s_[:, k:2560:20]))

    def sources(h):
        scan(X("s4", s_[:, 160 * h:160 * h + 160]), X("mk4"), X("wt", s_[:, 1280 * h:1280 * h + 1280:8]), 0.0, A.min, A.add)
        yield
        tt(X("u1", s_[0:64, 40 * h:40 * h + 40]), X("s4", s_[0:64, 160 * h + 3:160 * h + 160:4]), X("s4", s_[64:128, 160 * h + 3:160 * h + 160:4]), A.add)
        yield
        for a in range(4):
            k = slice(40 * h + a, 40 * h + 40, 4)
            tt(X("w3", s_[32 * a:32 * a + 32, 10 * h:10 * h + 10]), X("u1", s_[0:32, k]), X("u1", s_[32:64, k]), A.add)
        yield
        ts(X("gl", s_[:, 10 * h:10 * h + 10]), X("w3", s_[:, 10 * h:10 * h + 10]), CC, A.add)
        yield
        for b in (0, 2, 1, 3):
            o = X("yt", s_[:, 640 * h + b:640 * h + 640:4])
            i = by(X("tw", s_[:, 320 * b:320 * b + 10560]), X("gl", s_[:, 10 * h:10 * h + 10]))
            if b < OPT.get("gv", (2, 2))[h]:
                copy(o, i)
            else:
                act(o, i)
        yield
        for k in range(OPT.get("gy", 0) * h):
            yield

    def cross(t):
        yield from sources(1)
        out, land = Q("ac%d" % t, 0, 160), Q("lc%d" % t, 0, 160)
        quant(out, X("yt", s_[:, 640:1280]))
        dst = T.cores[rank ^ ROUNDS[t]]
        rid, pid = topo.addr(dst)[0:2]
        mask = 0
        for e in topo.engines(core, dst)[0:8]:
            mask |= 1 << e
        wait("p", need("p", feet(out), []))
        arr, snt = T.sem["arr%d" % t], T.sem["snt%d" % t]
        free = topo.engines(core, dst)
        if len(free) >= 16 and OPT.get("fuse"):
            sides = [(raw(X("lc%d" % t, s_[:, 40 * k:40 * k + 40]))[0], raw(X("ac%d" % t, s_[:, 40 * k:40 * k + 40]))[0]) for k in range(4)] + [(land[1][0], out[1][0])]
            cuts = [0, 4, 8, 12, 14, 16]
            g.remote_dma_fused([RemoteDMATransfer(dst_ids=[DstId(rid=rid, pnc=pid)], dma_engine_mask=sum(1 << e for e in free[cuts[k]:cuts[k + 1]]),
                                                  remote_sem=arr, src=i, dst=o) for k, (o, i) in enumerate(sides)], local_sem=snt)
        else:
            g.remote_dma(raw(land[0])[0], raw(out[0])[0], arr, snt, pid, rid, mask)
            g.remote_dma(land[1][0], out[1][0], arr, snt, pid, rid, mask)
        snap[("arr%d" % t, 16)] = {}
        note(("arr%d" % t, 16), [], feet(land))
        cnt["arr%d" % t] = cnt["snt%d" % t] = 16
        yield

    def stay_list(t):
        for ks in OPT.get("tk", ((), (0, 1, 2, 3), (4, 5, 6, 7), (8, 9)))[1:]:
            turns(ks)
            yield
        if t < 2:
            dmas("dz", [("s", X("win", s_[0:128:8, :]), X("win0"))])
        yield from sources(0)

    def layer_stay():
        yield
        quant(Q("zq", 0, 160), X("yt", s_[:, 0:640]))
        for b in (2, 3, 0, 1):
            act(X("y64", s_[:, b:640:4]), X("yt", s_[:, b:640:4]), 64.0)
        yield
        for b in (2, 3, 0, 1):
            p = mm(bank(), 160, Q("wq", 128 * b, 128 * b + 128), Q("zq", 0, 160))
            tt(X("t64", s_[:, 160 * b:160 * b + 160]), p, X("y64", s_[:, b:640:4]), A.add)
            act(X("xt", s_[:, b:640:4]), X("t64", s_[:, 160 * b:160 * b + 160]), 0.015625)
        yield

    def for_the_end():
        ts(X("pd"), X("ti", s_[:, 0:1]), 4, A.arith_shift_right)
        ts(X("c4"), CC, -160.0, A.add)
        yield
        quant(Q("vq", 0, 128), X("vt"))
        ts(X("ph"), X("pd"), 7.0, A.add)
        yield

    def numbers():
        ts(X("gi"), X("w3"), X("c4"), A.add, 0.00078125, A.mult)
        ts(X("n2"), X("w3"), CC, A.add, 8.0, A.mult)
        yield
        ts(X("gj"), X("gi"), X("ph"), A.add)
        ts(X("n4"), X("gi"), -10240.0, A.mult)
        ts(X("gk"), X("gj"), 7, A.bitwise_and)
        tt(X("n5"), X("n2"), X("n4"), A.add)
        yield
        tt(X("nn", s_[:, 0:20]), X("gk"), X("n5"), A.add)
        yield
        turn32(X("omt"), X("nn"))
        dmas("outs", [("s", hbm(T.om[c:c + 1, :]), X("omt", s_[32 * (c // 2):32 * (c // 2) + 20, 16 * (c % 2):16 * (c % 2) + 16])) for c in range(8)], False)
        yield

    def layer_arrived(t):
        land = Q("lc%d" % t, 0, 160)
        for b in range(4):
            k = bank()
            mm(k, 160, Q("wq", 128 * b, 128 * b + 128), land, True, False)
            p = mm(k, 160, Q("eq", EC * b, EC * b + 128), land, False, True)
            o = X("xt", s_[:, 640 + b:1280:4])
            if b in OPT["ev"][t]:
                ts(o, p, 0.015625, A.mult)
            else:
                act(o, p, 0.015625)

    def later(n, chain):
        for k in range(n):
            yield
        yield from chain

    follow(OPT["or0"], k=choose(0), r=choose(1), c=constants())
    for t in range(3):
        places(t)
        if t == 0:
            if OPT.get("wl", 0) == 1:
                dmas("dw", [("s", raw(X("wq")), hbm(T.wc[:])), ("s", X("wsc"), hbm(T.ws[:]))])
            dmas("dv", [("s", X("vt"), hbm(T.v[:]))])
        turns(range(10, 20))
        turns(OPT.get("tk", ((), (0, 1, 2, 3), (4, 5, 6, 7), (8, 9)))[0])
        weave(cross(t), stay_list(t))
        weave(layer_stay(), numbers() if t == 2 else for_the_end() if t == 0 else iter(()))
        if t < 2:
            layer_arrived(t)
            follow(OPT["ord"][t], k=choose(0), r=choose(1, window_early))

    quant(xh(0), X("xt", s_[:, 0:640]))
    layer_arrived(2)
    act(X("yo", s_[:, 0:160]), mm(0, 160, Q("vq", 0, 128), xh(0)))
    quant(xh(1), X("xt", s_[:, 640:1280]))
    copy(X("yo", s_[:, 160:320]), mm(1, 160, Q("vq", 0, 128), xh(1)))
    jobs = [("s", hbm(T.oc[:, 640 * h:640 * h + 640]), raw(xh(h)[0])) for h in range(2)]
    jobs += [("as"[h], hbm(T.y[:, 160 * h:160 * h + 160]), X("yo", s_[:, 160 * h:160 * h + 160])) for h in range(2)]
    jobs += [("a", hbm(T.osc[4 * k:4 * k + 4, :]), X("xs", s_[32 * k:32 * k + 4, :])) for k in range(4)]
    dmas("outs", jobs)
    for s in SEMAPHORES:
        if cnt.get(s, 0) > clock["p"].get(s, 0):
            g.wait_ge(T.sem[s], cnt[s])
